import numpy as np
import ml_dtypes


def mxq(x, axis, fmt="e4m3"):
    dtype, down = {"e4m3": (ml_dtypes.float8_e4m3fn, 7), "e5m2": (ml_dtypes.float8_e5m2, 14)}[fmt]
    v = np.moveaxis(np.asarray(x, np.float32).astype(ml_dtypes.bfloat16).astype(np.float64), axis, -1)
    blocks = v.reshape(v.shape[:-1] + (-1, 32))
    amax = np.abs(blocks).max(-1, keepdims=True)
    byte = np.maximum(np.where(amax > 0, np.frexp(amax)[1] - 1 + 127, 0) - down, 1)
    scale = np.exp2(byte - 127.0)
    codes = (blocks / scale).astype(np.float32).astype(dtype).astype(np.float64)
    return np.moveaxis((codes * scale).reshape(v.shape), -1, axis)


WIDE = False


def mx_kscale(k):
    if not WIDE:
        return np.ones(k)
    levels = np.array([10, -10, 5, -5, 0])
    if k % 512:
        return np.exp2(np.random.permutation(np.resize(levels, k // 32))).repeat(32)
    a = np.empty((k // 512, 16))
    for p in range(k // 512):
        a[p, :8] = np.random.permutation(np.resize(levels, 8))
        for g in range(8):
            far = levels[np.abs(levels - a[p, g]) >= 10]
            a[p, g + 8] = far[np.random.randint(len(far))]
    return np.exp2(a.ravel()).repeat(32)


def f64(x):
    return np.asarray(x).astype(np.float64)


def striped(idx):
    return np.tile(idx.reshape(-1, 16).T, (8, 1)).astype(np.uint16)


def unstriped(offs):
    return offs[:16].T.reshape(-1).astype(np.int64)


E2M1 = np.array([0.0, 0.5, 1.0, 1.5, 2.0, 3.0, 4.0, 6.0, -0.0, -0.5, -1.0, -1.5, -2.0, -3.0, -4.0, -6.0])


def pack_weight(w, fmt):
    k, n = w.shape
    w = f64(np.asarray(w, np.float32).astype(ml_dtypes.bfloat16)).reshape(k // 32, 32, n)
    amax = np.abs(w).max(1)
    if fmt == "e4m3":
        byte = np.frexp(amax)[1] - 1 + 127 - 7
    else:
        mant, ex = np.frexp(amax / 6.0)
        byte = np.where(mant > 0.5, ex, ex - 1) + 127
    byte = np.clip(np.where(amax > 0, byte, 1), 1, 254)
    scaled = (w * np.exp2(127.0 - byte)[:, None, :]).reshape(k, n).astype(np.float32)
    by_word = np.ascontiguousarray(scaled.reshape(k // 512, 128, 4, n).transpose(0, 1, 3, 2))
    if fmt == "e4m3":
        words = by_word.astype(ml_dtypes.float8_e4m3fn).view(np.uint8)
    else:
        c = by_word.astype(ml_dtypes.float4_e2m1fn).view(np.uint8) & 0xF
        words = (c[..., 0::2] | (c[..., 1::2] << 4)).reshape(k // 512, 128, 2 * n)
    return np.ascontiguousarray(words), np.ascontiguousarray(byte.astype(np.uint8).reshape(k // 512, 16, n))


def unpack_weight(words, scales, fmt):
    g, _, n = scales.shape
    words = np.ascontiguousarray(words).reshape(g, 128, n, -1)
    if fmt == "e4m3":
        vals = words.view(ml_dtypes.float8_e4m3fn).astype(np.float64)
    else:
        nib = np.empty((g, 128, n, 4), np.uint8)
        nib[..., 0::2] = words & 0xF
        nib[..., 1::2] = words >> 4
        vals = E2M1[nib]
    vals = vals * np.repeat(np.exp2(scales.astype(np.float64) - 127.0), 8, axis=1)[..., None]
    return vals.transpose(0, 1, 3, 2).reshape(g * 512, n)


def relu(v):
    return np.maximum(v, 0.0)


K, T, E, C, H, N = 512, 640, 4, 128, 512, 512


def by_expert(wq, xq):
    return np.concatenate([wq[e].T @ xq[:, e * C:(e + 1) * C] for e in range(E)], axis=1)


def setup_inputs():
    n = np.random.standard_normal
    s = mx_kscale(K)[:, None]
    u = mx_kscale(H)
    w1 = [pack_weight(m, "e2m1") for m in n((E, K, H)) / np.sqrt(K) / s[None]]
    w3 = [pack_weight(m, "e2m1") for m in n((E, K, H)) / np.sqrt(K) / s[None] * u[None, None, :]]
    w2 = [pack_weight(m, "e2m1") for m in n((E, H, N)) / np.sqrt(H) / u[None, :, None]]
    return {
        "xT": (n((K, T)) * s).astype(np.float32),
        "xr": n((N, T)).astype(np.float32),
        "w1_words": np.stack([m[0] for m in w1]),
        "w1_scales": np.stack([m[1] for m in w1]),
        "w3_words": np.stack([m[0] for m in w3]),
        "w3_scales": np.stack([m[1] for m in w3]),
        "w2_words": np.stack([m[0] for m in w2]),
        "w2_scales": np.stack([m[1] for m in w2]),
        "gate": np.tile(np.random.uniform(0.2, 1.0, E * C), (N, 1)).astype(np.float32),
        "offs": striped(np.random.permutation(T)[:E * C]),
    }


def reference(xT, xr, w1_words, w1_scales, w3_words, w3_scales, w2_words, w2_scales, gate, offs):
    idx = unstriped(offs)
    w1 = np.stack([unpack_weight(w1_words[e], w1_scales[e], "e2m1") for e in range(E)])
    w3 = np.stack([unpack_weight(w3_words[e], w3_scales[e], "e2m1") for e in range(E)])
    w2 = np.stack([unpack_weight(w2_words[e], w2_scales[e], "e2m1") for e in range(E)])
    xq = mxq(f64(xT)[:, idx], 0, "e4m3")
    h = relu(by_expert(w1, xq))
    h = h * by_expert(w3, xq)
    y = by_expert(w2, mxq(h, 0, "e4m3"))
    out = f64(xr).copy()
    out[:, idx] += f64(gate) * y
    return out

@@ -1,0 +1,239 @@
+from contextlib import ExitStack
+
+import concourse.mybir as mybir
+from concourse.masks import make_identity
+
+K, T, E, C, H, N = 512, 640, 4, 128, 512, 512
+P = 128
+UNIT = 128
+NT = N // P
+
+FLOPS = 3 * 2 * E * C * K * H
+BYTES = 2 * K * T * 4 + N * T * 4 + 3 * E * (P * 1024 + 16 * 512) + E * C * 4 + P * 64
+
+F32 = mybir.dt.float32
+BF16 = mybir.dt.bfloat16
+U32 = mybir.dt.uint32
+I32 = mybir.dt.int32
+U16 = mybir.dt.uint16
+U8 = mybir.dt.uint8
+FP8X4 = mybir.dt.float8_e4m3fn_x4
+FP4X4 = mybir.dt.float4_e2m1fn_x4
+ADD = mybir.AluOpType.add
+MULT = mybir.AluOpType.mult
+RELU = mybir.ActivationFunctionType.Relu
+COPY = mybir.ActivationFunctionType.Copy
+
+
+def tile_moe_res_glu_relu_kernel(
+    tc, xT, xr, w1_words, w1_scales, w3_words, w3_scales, w2_words, w2_scales, gate, offs, out
+):
+    nc = tc.nc
+    with ExitStack() as ctx:
+        held = ctx.enter_context(tc.tile_pool(name="held", bufs=1))
+        work = ctx.enter_context(tc.tile_pool(name="work", bufs=2))
+        ps2 = ctx.enter_context(tc.psum_pool(name="ps2", bufs=2))
+
+        offsets = held.tile([P, E * C // 16], U16, name="offsets")
+        gate_t = held.tile([P, 2 * C], F32, name="gate_t")
+        gate_col = held.tile([P, 2], F32, name="gate_col")
+        ident = held.tile([P, P], F32, name="ident")
+        warm = held.tile([P, 1], F32, name="warm")
+        codes = held.tile([P, T], U32, name="codes", align_bytes=64)
+        scales = held.tile([P, T], U8, name="scales", align_bytes=64)
+        gcodes = held.tile([P, E * C], U32, name="gcodes", align_bytes=64)
+        gscales = held.tile([P, E * C], U8, name="gscales", align_bytes=64)
+        w1w = held.tile([P, E, 2 * H], U8, name="w1w", align_bytes=64)
+        w3w = held.tile([P, E, 2 * H], U8, name="w3w", align_bytes=64)
+        w2w = held.tile([P, E, 2 * N], U8, name="w2w", align_bytes=64)
+        w1s = held.tile([P, E, H], U8, name="w1s", align_bytes=64)
+        w3s = held.tile([P, E, H], U8, name="w3s", align_bytes=64)
+        w2s = held.tile([P, E, N], U8, name="w2s", align_bytes=64)
+        res = held.tile([P, NT, T], F32, name="res")
+        chunk_cols = [(0, 384), (384, 640)]
+        raws = [held.tile([P, 4, b - a], F32, name=f"raw{a}") for a, b in chunk_cols]
+        yfull = [held.tile([P, T], F32, name=f"yfull{t}") for t in range(NT)]
+
+        for pl in (w1s, w3s, w2s):
+            nc.gpsimd.memset(pl[:].rearrange("p e i -> p (e i)").bitcast(I32), 0)
+        nc.gpsimd.memset(scales[:].bitcast(I32), 0)
+        make_identity(nc, ident[:])
+        nc.vector.memset(warm[:], 0.0)
+        for t in range(NT):
+            nc.vector.memset(yfull[t][:], 0.0)
+
+        x_rows = xT.rearrange("(p j) t -> p j t", j=4)
+
+        def load_scales(engine, plane, src, quads):
+            for q in quads:
+                engine.dma_start(
+                    plane[32 * q : 32 * q + 4, :, :].bitcast(I32),
+                    src[:, 0, 4 * q : 4 * q + 4, :].rearrange("e q i -> q e i").bitcast(I32),
+                )
+
+        def load_words(tile, src, a, b):
+            nc.sync.dma_start(tile[:, a:b, :].bitcast(I32), src[a:b, 0].rearrange("e p n -> p e n").bitcast(I32))
+
+        nc.sync.dma_start(offsets[:], offs)
+        load_scales(nc.scalar, w1s, w1_scales, (0, 1, 2, 3))
+        nc.scalar.activation(out=warm[:], in_=warm[:], func=RELU)
+        for raw, (a, b) in zip(raws, chunk_cols):
+            nc.sync.dma_start(raw[:], x_rows[:, :, a:b])
+        load_words(w1w, w1_words, 0, 1)
+        load_scales(nc.sync, w3s, w3_scales, (0, 1, 2, 3))
+        load_words(w3w, w3_words, 0, 1)
+        load_words(w1w, w1_words, 1, E)
+        load_words(w3w, w3_words, 1, E)
+        load_scales(nc.sync, w2s, w2_scales, (0, 1, 2, 3))
+        load_words(w2w, w2_words, 0, E)
+        nc.sync.dma_start(gate_t[:], gate[0:P, 0 : 2 * C])
+        with nc.allow_non_contiguous_dma(reason="one gate weight a partition"):
+            nc.sync.dma_start(gate_col[:], gate[0, 2 * C : 4 * C].rearrange("(e c) -> c e", e=2))
+        nc.sync.dma_start(res[:], xr.rearrange("(t p) c -> p t c", p=P))
+
+        for ci, a, b in ((0, 0, 256), (0, 256, 384), (1, 384, 640)):
+            grouped = held.tile([P, b - a, 4], BF16, name=f"grouped{a}", align_bytes=64)
+            for u in range(a, b, UNIT):
+                off = u - chunk_cols[ci][0]
+                src = raws[ci][:, :, off : off + UNIT].rearrange("p j w -> p w j")
+                dst = grouped[:, u - a : u - a + UNIT, :]
+                if u == a:
+                    nc.vector.tensor_copy(out=dst, in_=src)
+                else:
+                    nc.scalar.copy(out=dst, in_=src)
+            nc.vector.quantize_mx(
+                out=codes[:, a:b].bitcast(FP8X4),
+                scales=scales[:, a:b],
+                in_=grouped[:].rearrange("p w j -> p (w j)"),
+            )
+
+        def gather(e0, e1):
+            lst = offsets[:, e0 * 8 : e1 * 8]
+            nc.vector.tensor_copy(gcodes[:, e0 * C : e1 * C], codes[:].indirect(lst))
+            nc.vector.tensor_copy(gscales[:, e0 * C : e1 * C], scales[:].indirect(lst))
+
+        state = {}
+
+        def layer1(e):
+            cols = slice(e * C, (e + 1) * C)
+            pa = ps2.tile([P, H], F32, name="pa")
+            pb = ps2.tile([P, H], F32, name="pb")
+            for acc, words, sc in ((pa, w1w, w1s), (pb, w3w, w3s)):
+                nc.tensor.matmul_mx(
+                    out=acc[:],
+                    lhsT=gcodes[:, cols].bitcast(FP8X4),
+                    lhsT_scale=gscales[:, cols],
+                    rhs=words[:, e, :].bitcast(FP4X4),
+                    rhs_scale=sc[:, e, :],
+                    start=True,
+                    stop=True,
+                )
+            ra = work.tile([P, H], F32, name="ra")
+            nc.scalar.activation(out=ra[:], in_=pa[:], func=RELU)
+            h = work.tile([P, H], BF16, name="h")
+            nc.vector.tensor_tensor(out=h[:], in0=pb[:], in1=ra[:], op=MULT)
+            state[e] = h
+
+        def turn(e0, e1):
+            n = e1 - e0
+            ph = ps2.tile([P, n, 2, C], F32, name="ph")
+            for e in range(e0, e1):
+                pairs = state[e][:].bitcast(F32)
+                for u in range(2):
+                    nc.tensor.transpose(ph[:, e - e0, u, :], pairs[:, u::2], ident[:])
+            hg = work.tile([P, n, C, 4], BF16, name="hg", align_bytes=64)
+            nc.scalar.copy(
+                out=hg[:].rearrange("p e c j -> p (e c j)").bitcast(F32).rearrange("p (e c u) -> p e c u", e=n, u=2),
+                in_=ph[:].rearrange("p e u c -> p e c u"),
+            )
+            hc = work.tile([P, n * C], U32, name="hc", align_bytes=64)
+            hs = work.tile([P, n * C], U8, name="hs", align_bytes=64)
+            nc.vector.quantize_mx(
+                out=hc[:].bitcast(FP8X4), scales=hs[:], in_=hg[:].rearrange("p e c j -> p (e c j)")
+            )
+            for e in range(e0, e1):
+                cols = slice((e - e0) * C, (e - e0 + 1) * C)
+                state[e] = (hc[:, cols], hs[:, cols])
+
+        def layer2(e, dst):
+            hc, hs = state[e]
+            py = ps2.tile([P, NT, C], F32, name="py")
+            for t in range(NT):
+                nc.tensor.matmul_mx(
+                    out=py[:, t, :],
+                    lhsT=w2w[:, e, t * 2 * P : (t + 1) * 2 * P].bitcast(FP4X4),
+                    lhsT_scale=w2s[:, e, t * P : (t + 1) * P],
+                    rhs=hc.bitcast(FP8X4),
+                    rhs_scale=hs,
+                    start=True,
+                    stop=True,
+                )
+            nc.scalar.copy(out=dst, in_=py[:])
+
+        def layer2_turned(e):
+            hc, hs = state[e]
+            pz = ps2.tile([P, N], F32, name="pa")
+            nc.tensor.matmul_mx(
+                out=pz[:],
+                lhsT=hc.bitcast(FP8X4),
+                lhsT_scale=hs,
+                rhs=w2w[:, e, :].bitcast(FP4X4),
+                rhs_scale=w2s[:, e, :],
+                start=True,
+                stop=True,
+            )
+            yg = work.tile([P, N], F32, name="yg")
+            nc.scalar.activation(out=yg[:], in_=pz[:], func=COPY, scale=gate_col[:, e - 2 : e - 1])
+            state[e] = yg
+
+        def turn_back(e, dst):
+            yg = state[e]
+            pt = ps2.tile([P, NT, C], F32, name="pb")
+            for t in range(NT):
+                nc.tensor.transpose(pt[:, t, :], yg[:, t * P : (t + 1) * P], ident[:])
+            nc.scalar.copy(out=dst, in_=pt[:])
+
+        def scatter_plain(t, e0, e1, values):
+            nc.vector.tensor_copy(yfull[t][:].indirect(offsets[:, e0 * 8 : e1 * 8]), values)
+
+        def scatter(t, e0, e1, values):
+            nc.vector.tensor_tensor(
+                yfull[t][:].indirect(offsets[:, e0 * 8 : e1 * 8]), values, gate_t[:, e0 * C : e1 * C], MULT
+            )
+
+        y0 = held.tile([P, NT, C], F32, name="y0")
+        y1 = held.tile([P, NT, C], F32, name="y1")
+        y23 = held.tile([P, NT, 2, C], F32, name="y23")
+        dsts = [y0[:], y1[:], y23[:, :, 0, :], y23[:, :, 1, :]]
+
+        gather(0, 1)
+        layer1(0)
+        gather(1, 4)
+        layer1(1)
+        turn(0, 1)
+        layer1(2)
+        layer2(0, dsts[0])
+        turn(1, 2)
+        layer1(3)
+        layer2(1, dsts[1])
+        turn(2, 4)
+        layer2_turned(2)
+        layer2_turned(3)
+        turn_back(2, dsts[2])
+        turn_back(3, dsts[3])
+        for t in range(NT):
+            scatter(t, 0, 1, y0[:, t, :])
+        for t in range(NT):
+            scatter(t, 1, 2, y1[:, t, :])
+        def finish(t):
+            o = work.tile([P, T], F32, name="o", bufs=NT)
+            engine = nc.vector if t == NT - 1 else nc.gpsimd
+            step = T // 2 if t == NT - 1 else T
+            for a in range(0, T, step):
+                cols = slice(a, a + step)
+                engine.tensor_tensor(out=o[:, cols], in0=yfull[t][:, cols], in1=res[:, t, cols], op=ADD)
+                nc.sync.dma_start(out[t * P : (t + 1) * P, cols], o[:, cols])
+
+        for t in range(NT):
+            scatter_plain(t, 2, 4, y23[:, t, :, :].rearrange("p e c -> p (e c)"))
+            finish(t)

@@ -5,8 +5,8 @@ from concourse.masks import make_identity
 
 K, T, E, C, H, N = 512, 640, 4, 128, 512, 512
 P = 128
-UNIT = 128
 NT = N // P
+WINDOW = 768
 
 FLOPS = 3 * 2 * E * C * K * H
 BYTES = 2 * K * T * 4 + N * T * 4 + 3 * E * (P * 1024 + 16 * 512) + E * C * 4 + P * 64
@@ -22,7 +22,6 @@ FP4X4 = mybir.dt.float4_e2m1fn_x4
 ADD = mybir.AluOpType.add
 MULT = mybir.AluOpType.mult
 RELU = mybir.ActivationFunctionType.Relu
-COPY = mybir.ActivationFunctionType.Copy
 
 
 def tile_moe_res_glu_relu_kernel(
@@ -32,19 +31,19 @@ def tile_moe_res_glu_relu_kernel(
     with ExitStack() as ctx:
         held = ctx.enter_context(tc.tile_pool(name="held", bufs=1))
         work = ctx.enter_context(tc.tile_pool(name="work", bufs=2))
-        ps2 = ctx.enter_context(tc.psum_pool(name="ps2", bufs=2))
+        psum = ctx.enter_context(tc.psum_pool(name="psum", bufs=1))
+        banks = [psum.tile([P, 512], F32, name=f"bank{i}") for i in range(8)]
 
         offsets = held.tile([P, E * C // 16], U16, name="offsets")
-        gate_t = held.tile([P, 2 * C], F32, name="gate_t")
-        gate_col = held.tile([P, 2], F32, name="gate_col")
+        gate_t = held.tile([P, E * C], F32, name="gate_t")
         ident = held.tile([P, P], F32, name="ident")
         warm = held.tile([P, 1], F32, name="warm")
         codes = held.tile([P, T], U32, name="codes", align_bytes=64)
         scales = held.tile([P, T], U8, name="scales", align_bytes=64)
         gcodes = held.tile([P, E * C], U32, name="gcodes", align_bytes=64)
         gscales = held.tile([P, E * C], U8, name="gscales", align_bytes=64)
-        w1w = held.tile([P, E, 2 * H], U8, name="w1w", align_bytes=64)
-        w3w = held.tile([P, E, 2 * H], U8, name="w3w", align_bytes=64)
+        w1w = [held.tile([P, 2, 2 * H], U8, name=f"w1w{g}", align_bytes=64) for g in range(2)]
+        w3w = [held.tile([P, 2, 2 * H], U8, name=f"w3w{g}", align_bytes=64) for g in range(2)]
         w2w = held.tile([P, E, 2 * N], U8, name="w2w", align_bytes=64)
         w1s = held.tile([P, E, H], U8, name="w1s", align_bytes=64)
         w3s = held.tile([P, E, H], U8, name="w3s", align_bytes=64)
@@ -52,60 +51,68 @@ def tile_moe_res_glu_relu_kernel(
         res = held.tile([P, NT, T], F32, name="res")
         chunk_cols = [(0, 384), (384, 640)]
         raws = [held.tile([P, 4, b - a], F32, name=f"raw{a}") for a, b in chunk_cols]
-        yfull = [held.tile([P, T], F32, name=f"yfull{t}") for t in range(NT)]
+        windows = [held.tile([P, WINDOW], F32, name=f"window{t}") for t in range(NT)]
 
-        for pl in (w1s, w3s, w2s):
-            nc.gpsimd.memset(pl[:].rearrange("p e i -> p (e i)").bitcast(I32), 0)
         nc.gpsimd.memset(scales[:].bitcast(I32), 0)
         make_identity(nc, ident[:])
         nc.vector.memset(warm[:], 0.0)
         for t in range(NT):
-            nc.vector.memset(yfull[t][:], 0.0)
+            nc.vector.memset(windows[t][:, 0:T], 0.0)
 
         x_rows = xT.rearrange("(p j) t -> p j t", j=4)
 
-        def load_scales(engine, plane, src, quads):
-            for q in quads:
+        def load_scales(engine, plane, src):
+            for q in range(4):
                 engine.dma_start(
                     plane[32 * q : 32 * q + 4, :, :].bitcast(I32),
                     src[:, 0, 4 * q : 4 * q + 4, :].rearrange("e q i -> q e i").bitcast(I32),
                 )
 
         def load_words(tile, src, a, b):
-            nc.sync.dma_start(tile[:, a:b, :].bitcast(I32), src[a:b, 0].rearrange("e p n -> p e n").bitcast(I32))
+            nc.sync.dma_start(tile[:].bitcast(I32), src[a:b, 0].rearrange("e p n -> p e n").bitcast(I32))
 
-        nc.sync.dma_start(offsets[:], offs)
-        load_scales(nc.scalar, w1s, w1_scales, (0, 1, 2, 3))
+        def load_x(c):
+            a, b = chunk_cols[c]
+            nc.sync.dma_start(raws[c][:], x_rows[:, :, a:b])
+
         nc.scalar.activation(out=warm[:], in_=warm[:], func=RELU)
-        for raw, (a, b) in zip(raws, chunk_cols):
-            nc.sync.dma_start(raw[:], x_rows[:, :, a:b])
-        load_words(w1w, w1_words, 0, 1)
-        load_scales(nc.sync, w3s, w3_scales, (0, 1, 2, 3))
-        load_words(w3w, w3_words, 0, 1)
-        load_words(w1w, w1_words, 1, E)
-        load_words(w3w, w3_words, 1, E)
-        load_scales(nc.sync, w2s, w2_scales, (0, 1, 2, 3))
+        load_x(0)
+        load_x(1)
+        nc.sync.dma_start(offsets[:], offs)
+        load_scales(nc.sync, w1s, w1_scales)
+        load_words(w1w[0], w1_words, 0, 2)
+        load_words(w3w[0], w3_words, 0, 2)
+        load_scales(nc.sync, w3s, w3_scales)
+        load_words(w1w[1], w1_words, 2, 4)
+        load_words(w3w[1], w3_words, 2, 4)
         load_words(w2w, w2_words, 0, E)
-        nc.sync.dma_start(gate_t[:], gate[0:P, 0 : 2 * C])
-        with nc.allow_non_contiguous_dma(reason="one gate weight a partition"):
-            nc.sync.dma_start(gate_col[:], gate[0, 2 * C : 4 * C].rearrange("(e c) -> c e", e=2))
+        load_scales(nc.sync, w2s, w2_scales)
+        nc.sync.dma_start(gate_t[:], gate[0:P, :])
         nc.sync.dma_start(res[:], xr.rearrange("(t p) c -> p t c", p=P))
 
-        for ci, a, b in ((0, 0, 256), (0, 256, 384), (1, 384, 640)):
-            grouped = held.tile([P, b - a, 4], BF16, name=f"grouped{a}", align_bytes=64)
-            for u in range(a, b, UNIT):
-                off = u - chunk_cols[ci][0]
-                src = raws[ci][:, :, off : off + UNIT].rearrange("p j w -> p w j")
-                dst = grouped[:, u - a : u - a + UNIT, :]
-                if u == a:
-                    nc.vector.tensor_copy(out=dst, in_=src)
-                else:
-                    nc.scalar.copy(out=dst, in_=src)
+        def cast(engine_copy, grouped, g0, raw, r0, width):
+            engine_copy(
+                out=grouped[:, g0 : g0 + width, :], in_=raw[:, :, r0 : r0 + width].rearrange("p j w -> p w j")
+            )
+
+        def quantise(grouped, a, b):
             nc.vector.quantize_mx(
                 out=codes[:, a:b].bitcast(FP8X4),
                 scales=scales[:, a:b],
                 in_=grouped[:].rearrange("p w j -> p (w j)"),
             )
+
+        g0 = held.tile([P, 256, 4], BF16, name="grouped0", align_bytes=64)
+        g1 = held.tile([P, 128, 4], BF16, name="grouped1", align_bytes=64)
+        g2 = held.tile([P, 256, 4], BF16, name="grouped2", align_bytes=64)
+        cast(nc.vector.tensor_copy, g0, 0, raws[0], 0, 224)
+        cast(nc.scalar.copy, g0, 224, raws[0], 224, 32)
+        cast(nc.scalar.copy, g1, 0, raws[0], 256, 128)
+        quantise(g0, 0, 256)
+        quantise(g1, 256, 384)
+        cast(nc.vector.tensor_copy, g2, 0, raws[1], 0, 160)
+        cast(nc.scalar.copy, g2, 160, raws[1], 160, 96)
+        quantise(g2, 384, 640)
 
         def gather(e0, e1):
             lst = offsets[:, e0 * 8 : e1 * 8]
@@ -116,14 +123,14 @@ def tile_moe_res_glu_relu_kernel(
 
         def layer1(e):
             cols = slice(e * C, (e + 1) * C)
-            pa = ps2.tile([P, H], F32, name="pa")
-            pb = ps2.tile([P, H], F32, name="pb")
+            pa = banks[2 * (e % 2)]
+            pb = banks[2 * (e % 2) + 1]
             for acc, words, sc in ((pa, w1w, w1s), (pb, w3w, w3s)):
                 nc.tensor.matmul_mx(
                     out=acc[:],
                     lhsT=gcodes[:, cols].bitcast(FP8X4),
                     lhsT_scale=gscales[:, cols],
-                    rhs=words[:, e, :].bitcast(FP4X4),
+                    rhs=words[e // 2][:, e % 2, :].bitcast(FP4X4),
                     rhs_scale=sc[:, e, :],
                     start=True,
                     stop=True,
@@ -134,9 +141,9 @@ def tile_moe_res_glu_relu_kernel(
             nc.vector.tensor_tensor(out=h[:], in0=pb[:], in1=ra[:], op=MULT)
             state[e] = h
 
-        def turn(e0, e1):
+        def turn(e0, e1, bank):
             n = e1 - e0
-            ph = ps2.tile([P, n, 2, C], F32, name="ph")
+            ph = bank[:, 0 : n * 2 * C].rearrange("p (e u c) -> p e u c", e=n, u=2)
             for e in range(e0, e1):
                 pairs = state[e][:].bitcast(F32)
                 for u in range(2):
@@ -144,7 +151,7 @@ def tile_moe_res_glu_relu_kernel(
             hg = work.tile([P, n, C, 4], BF16, name="hg", align_bytes=64)
             nc.scalar.copy(
                 out=hg[:].rearrange("p e c j -> p (e c j)").bitcast(F32).rearrange("p (e c u) -> p e c u", e=n, u=2),
-                in_=ph[:].rearrange("p e u c -> p e c u"),
+                in_=ph.rearrange("p e u c -> p e c u"),
             )
             hc = work.tile([P, n * C], U32, name="hc", align_bytes=64)
             hs = work.tile([P, n * C], U8, name="hs", align_bytes=64)
@@ -155,12 +162,17 @@ def tile_moe_res_glu_relu_kernel(
                 cols = slice((e - e0) * C, (e - e0 + 1) * C)
                 state[e] = (hc[:, cols], hs[:, cols])
 
-        def layer2(e, dst):
+        y0 = held.tile([P, NT, C], F32, name="y0")
+        y1_low = held.tile([P, 2, C], F32, name="y1_low")
+        y23_low = held.tile([P, 2, 2, C], F32, name="y23_low")
+        y123_high = held.tile([P, 2, 3, C], F32, name="y123_high")
+
+        def layer2(e, t0, t1, bank):
             hc, hs = state[e]
-            py = ps2.tile([P, NT, C], F32, name="py")
-            for t in range(NT):
+            py = bank[:, 0 : (t1 - t0) * C].rearrange("p (t c) -> p t c", c=C)
+            for t in range(t0, t1):
                 nc.tensor.matmul_mx(
-                    out=py[:, t, :],
+                    out=py[:, t - t0, :],
                     lhsT=w2w[:, e, t * 2 * P : (t + 1) * 2 * P].bitcast(FP4X4),
                     lhsT_scale=w2s[:, e, t * P : (t + 1) * P],
                     rhs=hc.bitcast(FP8X4),
@@ -168,72 +180,86 @@ def tile_moe_res_glu_relu_kernel(
                     start=True,
                     stop=True,
                 )
-            nc.scalar.copy(out=dst, in_=py[:])
+            return py
 
-        def layer2_turned(e):
-            hc, hs = state[e]
-            pz = ps2.tile([P, N], F32, name="pa")
-            nc.tensor.matmul_mx(
-                out=pz[:],
-                lhsT=hc.bitcast(FP8X4),
-                lhsT_scale=hs,
-                rhs=w2w[:, e, :].bitcast(FP4X4),
-                rhs_scale=w2s[:, e, :],
-                start=True,
-                stop=True,
-            )
-            yg = work.tile([P, N], F32, name="yg")
-            nc.scalar.activation(out=yg[:], in_=pz[:], func=COPY, scale=gate_col[:, e - 2 : e - 1])
-            state[e] = yg
-
-        def turn_back(e, dst):
-            yg = state[e]
-            pt = ps2.tile([P, NT, C], F32, name="pb")
-            for t in range(NT):
-                nc.tensor.transpose(pt[:, t, :], yg[:, t * P : (t + 1) * P], ident[:])
-            nc.scalar.copy(out=dst, in_=pt[:])
-
-        def scatter_plain(t, e0, e1, values):
-            nc.vector.tensor_copy(yfull[t][:].indirect(offsets[:, e0 * 8 : e1 * 8]), values)
-
-        def scatter(t, e0, e1, values):
+        def scatter(t, e0, e1):
+            if e0 == 0:
+                values = y0[:, t, :]
+            elif e1 == 2:
+                values = y1_low[:, t, :]
+            elif e0 == 2:
+                values = y23_low[:, t, :, :].rearrange("p e c -> p (e c)")
+            else:
+                values = y123_high[:, t - 2, :, :].rearrange("p e c -> p (e c)")
             nc.vector.tensor_tensor(
-                yfull[t][:].indirect(offsets[:, e0 * 8 : e1 * 8]), values, gate_t[:, e0 * C : e1 * C], MULT
+                windows[t][:].indirect(offsets[:, e0 * 8 : e1 * 8]),
+                values,
+                gate_t[:, e0 * C : e1 * C],
+                MULT,
             )
 
-        y0 = held.tile([P, NT, C], F32, name="y0")
-        y1 = held.tile([P, NT, C], F32, name="y1")
-        y23 = held.tile([P, NT, 2, C], F32, name="y23")
-        dsts = [y0[:], y1[:], y23[:, :, 0, :], y23[:, :, 1, :]]
+        def add_by_tensor(t, first, second):
+            o = work.tile([P, T], F32, name="o", bufs=NT)
+            parts = ((0, 3), (3, 5))
+            turned = []
+            for (b0, b1), bank in zip(parts, first):
+                n = b1 - b0
+                p1 = bank[:, 0 : n * P].rearrange("p (b c) -> p b c", c=P)
+                for b in range(b0, b1):
+                    nc.tensor.matmul(
+                        p1[:, b - b0, :], res[:, t, b * P : (b + 1) * P], ident[:],
+                        start=(b == b0), stop=False, is_transpose=True,
+                    )
+                for b in range(b0, b1):
+                    nc.tensor.matmul(
+                        p1[:, b - b0, :], windows[t][:, b * P : (b + 1) * P], ident[:],
+                        start=False, stop=(b == b1 - 1), is_transpose=True,
+                    )
+                s1 = work.tile([P, n, P], F32, name="s1")
+                nc.scalar.copy(out=s1[:], in_=p1)
+                turned.append(s1)
+            for (b0, b1), s1, bank in zip(parts, turned, second):
+                n = b1 - b0
+                for b in range(n):
+                    nc.tensor.transpose(bank[:, b * P : (b + 1) * P], s1[:, b, :], ident[:])
+                nc.scalar.copy(out=o[:, b0 * P : b1 * P], in_=bank[:, 0 : n * P])
+            nc.sync.dma_start(out[t * P : (t + 1) * P, :], o[:])
+
+        def add_by_vector(t):
+            o = work.tile([P, T], F32, name="o", bufs=NT)
+            for a in range(0, T, T // 2):
+                cols = slice(a, a + T // 2)
+                nc.vector.tensor_tensor(out=o[:, cols], in0=windows[t][:, cols], in1=res[:, t, cols], op=ADD)
+                nc.sync.dma_start(out[t * P : (t + 1) * P, cols], o[:, cols])
 
         gather(0, 1)
         layer1(0)
-        gather(1, 4)
+        gather(1, 2)
         layer1(1)
-        turn(0, 1)
+        gather(2, 4)
+        turn(0, 1, banks[4])
         layer1(2)
-        layer2(0, dsts[0])
-        turn(1, 2)
+        for t0, t1, bank in ((0, 1, banks[6]), (1, NT, banks[7])):
+            nc.scalar.copy(out=y0[:, t0:t1, :], in_=layer2(0, t0, t1, bank))
+        turn(1, 2, banks[5])
         layer1(3)
-        layer2(1, dsts[1])
-        turn(2, 4)
-        layer2_turned(2)
-        layer2_turned(3)
-        turn_back(2, dsts[2])
-        turn_back(3, dsts[3])
+        turn(2, 4, banks[6])
+        py1 = layer2(1, 0, NT, banks[6])
+        nc.scalar.copy(out=y1_low[:], in_=py1[:, 0:2, :])
+        nc.scalar.copy(out=y123_high[:, :, 0, :], in_=py1[:, 2:4, :])
+        py23 = [layer2(e, 0, NT, bank) for e, bank in ((2, banks[5]), (3, banks[7]))]
+        for e in (2, 3):
+            nc.scalar.copy(out=y23_low[:, :, e - 2, :], in_=py23[e - 2][:, 0:2, :])
+        for e in (2, 3):
+            nc.scalar.copy(out=y123_high[:, :, e - 1, :], in_=py23[e - 2][:, 2:4, :])
         for t in range(NT):
-            scatter(t, 0, 1, y0[:, t, :])
+            scatter(t, 0, 1)
+        for t in range(2):
+            scatter(t, 1, 2)
+        add_banks = (((5, 7), (0, 1)), ((2, 3), (4, 6)), ((5, 7), (0, 1)))
         for t in range(NT):
-            scatter(t, 1, 2, y1[:, t, :])
-        def finish(t):
-            o = work.tile([P, T], F32, name="o", bufs=NT)
-            engine = nc.vector if t == NT - 1 else nc.gpsimd
-            step = T // 2 if t == NT - 1 else T
-            for a in range(0, T, step):
-                cols = slice(a, a + step)
-                engine.tensor_tensor(out=o[:, cols], in0=yfull[t][:, cols], in1=res[:, t, cols], op=ADD)
-                nc.sync.dma_start(out[t * P : (t + 1) * P, cols], o[:, cols])
-
-        for t in range(NT):
-            scatter_plain(t, 2, 4, y23[:, t, :, :].rearrange("p e c -> p (e c)"))
-            finish(t)
+            scatter(t, 2 if t < 2 else 1, E)
+            if t < NT - 1:
+                add_by_tensor(t, [banks[i] for i in add_banks[t][0]], [banks[i] for i in add_banks[t][1]])
+            else:
+                add_by_vector(t)

@@ -49,7 +49,7 @@ def tile_moe_res_glu_relu_kernel(
         w3s = held.tile([P, E, H], U8, name="w3s", align_bytes=64)
         w2s = held.tile([P, E, N], U8, name="w2s", align_bytes=64)
         res = held.tile([P, NT, T], F32, name="res")
-        chunk_cols = [(0, 384), (384, 640)]
+        chunk_cols = [(0, 256), (256, 512), (512, 640)]
         raws = [held.tile([P, 4, b - a], F32, name=f"raw{a}") for a, b in chunk_cols]
         windows = [held.tile([P, WINDOW], F32, name=f"window{t}") for t in range(NT)]
 
@@ -77,8 +77,9 @@ def tile_moe_res_glu_relu_kernel(
 
         nc.scalar.activation(out=warm[:], in_=warm[:], func=RELU)
         load_x(0)
-        load_x(1)
         nc.sync.dma_start(offsets[:], offs)
+        load_x(1)
+        load_x(2)
         load_scales(nc.sync, w1s, w1_scales)
         load_words(w1w[0], w1_words, 0, 2)
         load_words(w3w[0], w3_words, 0, 2)
@@ -102,17 +103,12 @@ def tile_moe_res_glu_relu_kernel(
                 in_=grouped[:].rearrange("p w j -> p (w j)"),
             )
 
-        g0 = held.tile([P, 256, 4], BF16, name="grouped0", align_bytes=64)
-        g1 = held.tile([P, 128, 4], BF16, name="grouped1", align_bytes=64)
-        g2 = held.tile([P, 256, 4], BF16, name="grouped2", align_bytes=64)
-        cast(nc.vector.tensor_copy, g0, 0, raws[0], 0, 224)
-        cast(nc.scalar.copy, g0, 224, raws[0], 224, 32)
-        cast(nc.scalar.copy, g1, 0, raws[0], 256, 128)
-        quantise(g0, 0, 256)
-        quantise(g1, 256, 384)
-        cast(nc.vector.tensor_copy, g2, 0, raws[1], 0, 160)
-        cast(nc.scalar.copy, g2, 160, raws[1], 160, 96)
-        quantise(g2, 384, 640)
+        for raw, (a, b) in zip(raws, chunk_cols):
+            grouped = held.tile([P, b - a, 4], BF16, name=f"grouped{a}", align_bytes=64)
+            share = (b - a) * 5 // 8
+            cast(nc.vector.tensor_copy, grouped, 0, raw, 0, share)
+            cast(nc.scalar.copy, grouped, share, raw, share, b - a - share)
+            quantise(grouped, a, b)
 
         def gather(e0, e1):
             lst = offsets[:, e0 * 8 : e1 * 8]
@@ -136,18 +132,26 @@ def tile_moe_res_glu_relu_kernel(
                     stop=True,
                 )
             ra = work.tile([P, H], F32, name="ra")
-            nc.scalar.activation(out=ra[:], in_=pa[:], func=RELU)
-            h = work.tile([P, H], BF16, name="h")
-            nc.vector.tensor_tensor(out=h[:], in0=pb[:], in1=ra[:], op=MULT)
+            h = work.tile([P, 2, P, 2], BF16, name="h")
+            step = H // 2 if e == 0 else H
+            for i0 in range(0, H, step):
+                part = slice(i0, i0 + step)
+                nc.scalar.activation(out=ra[:, part], in_=pa[:, part], func=RELU)
+                nc.vector.tensor_tensor(
+                    out=h[:, :, i0 // 4 : (i0 + step) // 4, :].rearrange("s u p d -> s p u d"),
+                    in0=pb[:, part].rearrange("s (p u d) -> s p u d", u=2, d=2),
+                    in1=ra[:, part].rearrange("s (p u d) -> s p u d", u=2, d=2),
+                    op=MULT,
+                )
             state[e] = h
 
         def turn(e0, e1, bank):
             n = e1 - e0
             ph = bank[:, 0 : n * 2 * C].rearrange("p (e u c) -> p e u c", e=n, u=2)
             for e in range(e0, e1):
-                pairs = state[e][:].bitcast(F32)
                 for u in range(2):
-                    nc.tensor.transpose(ph[:, e - e0, u, :], pairs[:, u::2], ident[:])
+                    pairs = state[e][:, u, :, :].rearrange("s p d -> s (p d)").bitcast(F32)
+                    nc.tensor.transpose(ph[:, e - e0, u, :], pairs, ident[:])
             hg = work.tile([P, n, C, 4], BF16, name="hg", align_bytes=64)
             nc.scalar.copy(
                 out=hg[:].rearrange("p e c j -> p (e c j)").bitcast(F32).rearrange("p (e c u) -> p e c u", e=n, u=2),
@@ -162,10 +166,10 @@ def tile_moe_res_glu_relu_kernel(
                 cols = slice((e - e0) * C, (e - e0 + 1) * C)
                 state[e] = (hc[:, cols], hs[:, cols])
 
-        y0 = held.tile([P, NT, C], F32, name="y0")
-        y1_low = held.tile([P, 2, C], F32, name="y1_low")
-        y23_low = held.tile([P, 2, 2, C], F32, name="y23_low")
-        y123_high = held.tile([P, 2, 3, C], F32, name="y123_high")
+        y0 = held.tile([P, 3, C], F32, name="y0")
+        y1 = held.tile([P, 2, C], F32, name="y1")
+        y23 = held.tile([P, 2, 2, C], F32, name="y23")
+        y_high = held.tile([P, 2, E, C], F32, name="y_high")
 
         def layer2(e, t0, t1, bank):
             hc, hs = state[e]
@@ -182,15 +186,7 @@ def tile_moe_res_glu_relu_kernel(
                 )
             return py
 
-        def scatter(t, e0, e1):
-            if e0 == 0:
-                values = y0[:, t, :]
-            elif e1 == 2:
-                values = y1_low[:, t, :]
-            elif e0 == 2:
-                values = y23_low[:, t, :, :].rearrange("p e c -> p (e c)")
-            else:
-                values = y123_high[:, t - 2, :, :].rearrange("p e c -> p (e c)")
+        def scatter(t, e0, e1, values):
             nc.vector.tensor_tensor(
                 windows[t][:].indirect(offsets[:, e0 * 8 : e1 * 8]),
                 values,
@@ -239,27 +235,29 @@ def tile_moe_res_glu_relu_kernel(
         gather(2, 4)
         turn(0, 1, banks[4])
         layer1(2)
-        for t0, t1, bank in ((0, 1, banks[6]), (1, NT, banks[7])):
-            nc.scalar.copy(out=y0[:, t0:t1, :], in_=layer2(0, t0, t1, bank))
+        nc.scalar.copy(out=y0[:, 0:1, :], in_=layer2(0, 0, 1, banks[6]))
+        py0 = layer2(0, 1, NT, banks[7])
+        nc.scalar.copy(out=y0[:, 1:3, :], in_=py0[:, 0:2, :])
+        nc.scalar.copy(out=y_high[:, 1, 0, :], in_=py0[:, 2, :])
         turn(1, 2, banks[5])
         layer1(3)
         turn(2, 4, banks[6])
         py1 = layer2(1, 0, NT, banks[6])
-        nc.scalar.copy(out=y1_low[:], in_=py1[:, 0:2, :])
-        nc.scalar.copy(out=y123_high[:, :, 0, :], in_=py1[:, 2:4, :])
+        nc.scalar.copy(out=y1[:], in_=py1[:, 0:2, :])
+        nc.scalar.copy(out=y_high[:, :, 1, :], in_=py1[:, 2:4, :])
         py23 = [layer2(e, 0, NT, bank) for e, bank in ((2, banks[5]), (3, banks[7]))]
         for e in (2, 3):
-            nc.scalar.copy(out=y23_low[:, :, e - 2, :], in_=py23[e - 2][:, 0:2, :])
+            nc.scalar.copy(out=y23[:, :, e - 2, :], in_=py23[e - 2][:, 0:2, :])
         for e in (2, 3):
-            nc.scalar.copy(out=y123_high[:, :, e - 1, :], in_=py23[e - 2][:, 2:4, :])
-        for t in range(NT):
-            scatter(t, 0, 1)
+            nc.scalar.copy(out=y_high[:, :, e, :], in_=py23[e - 2][:, 2:4, :])
+        for t in range(3):
+            scatter(t, 0, 1, y0[:, t, :])
         for t in range(2):
-            scatter(t, 1, 2)
-        add_banks = (((5, 7), (0, 1)), ((2, 3), (4, 6)), ((5, 7), (0, 1)))
-        for t in range(NT):
-            scatter(t, 2 if t < 2 else 1, E)
-            if t < NT - 1:
-                add_by_tensor(t, [banks[i] for i in add_banks[t][0]], [banks[i] for i in add_banks[t][1]])
-            else:
-                add_by_vector(t)
+            scatter(t, 1, 2, y1[:, t, :])
+        for t, first, second in ((0, (5, 7), (0, 1)), (1, (2, 3), (4, 6))):
+            scatter(t, 2, E, y23[:, t, :, :].rearrange("p e c -> p (e c)"))
+            add_by_tensor(t, [banks[i] for i in first], [banks[i] for i in second])
+        scatter(2, 1, E, y_high[:, 0, 1:E, :].rearrange("p e c -> p (e c)"))
+        add_by_tensor(2, [banks[0], banks[1]], [banks[5], banks[7]])
+        scatter(3, 0, E, y_high[:, 1, :, :].rearrange("p e c -> p (e c)"))
+        add_by_vector(3)

@@ -211,15 +211,16 @@ def tile_moe_res_glu_relu_kernel(
                         p1[:, b - b0, :], windows[t][:, b * P : (b + 1) * P], ident[:],
                         start=False, stop=(b == b1 - 1), is_transpose=True,
                     )
-                s1 = work.tile([P, n, P], F32, name="s1")
+                s1 = work.tile([P, n, P], F32, name="s1", bufs=4)
                 nc.scalar.copy(out=s1[:], in_=p1)
                 turned.append(s1)
             for (b0, b1), s1, bank in zip(parts, turned, second):
                 n = b1 - b0
                 for b in range(n):
                     nc.tensor.transpose(bank[:, b * P : (b + 1) * P], s1[:, b, :], ident[:])
-                nc.scalar.copy(out=o[:, b0 * P : b1 * P], in_=bank[:, 0 : n * P])
-            nc.sync.dma_start(out[t * P : (t + 1) * P, :], o[:])
+                cols = slice(b0 * P, b1 * P)
+                nc.scalar.copy(out=o[:, cols], in_=bank[:, 0 : n * P])
+                nc.sync.dma_start(out[t * P : (t + 1) * P, cols], o[:, cols])
 
         def add_by_vector(t):
             o = work.tile([P, T], F32, name="o", bufs=NT)
@@ -254,10 +255,10 @@ def tile_moe_res_glu_relu_kernel(
             scatter(t, 0, 1, y0[:, t, :])
         for t in range(2):
             scatter(t, 1, 2, y1[:, t, :])
-        for t, first, second in ((0, (5, 7), (0, 1)), (1, (2, 3), (4, 6))):
+        for t, first, second in ((0, (0, 1), (5, 7)), (1, (2, 3), (0, 1))):
             scatter(t, 2, E, y23[:, t, :, :].rearrange("p e c -> p (e c)"))
             add_by_tensor(t, [banks[i] for i in first], [banks[i] for i in second])
         scatter(2, 1, E, y_high[:, 0, 1:E, :].rearrange("p e c -> p (e c)"))
-        add_by_tensor(2, [banks[0], banks[1]], [banks[5], banks[7]])
+        add_by_tensor(2, [banks[4], banks[6]], [banks[2], banks[3]])
         scatter(3, 0, E, y_high[:, 1, :, :].rearrange("p e c -> p (e c)"))
         add_by_vector(3)

@@ -93,7 +93,8 @@ def tile_moe_res_glu_relu_kernel(
 
         def cast(engine_copy, grouped, g0, raw, r0, width):
             engine_copy(
-                out=grouped[:, g0 : g0 + width, :], in_=raw[:, :, r0 : r0 + width].rearrange("p j w -> p w j")
+                out=grouped[:, g0 : g0 + width, :].rearrange("p (c i) j -> p c j i", i=4),
+                in_=raw[:, :, r0 : r0 + width].rearrange("p j (c i) -> p c j i", i=4),
             )
 
         def quantise(grouped, a, b):
@@ -224,10 +225,9 @@ def tile_moe_res_glu_relu_kernel(
 
         def add_by_vector(t):
             o = work.tile([P, T], F32, name="o", bufs=NT)
-            for a in range(0, T, T // 2):
-                cols = slice(a, a + T // 2)
+            for cols, queue in ((slice(0, 384), nc.sync), (slice(384, T), nc.scalar)):
                 nc.vector.tensor_tensor(out=o[:, cols], in0=windows[t][:, cols], in1=res[:, t, cols], op=ADD)
-                nc.sync.dma_start(out[t * P : (t + 1) * P, cols], o[:, cols])
+                queue.dma_start(out[t * P : (t + 1) * P, cols], o[:, cols])
 
         gather(0, 1)
         layer1(0)

@@ -76,10 +76,9 @@ def tile_moe_res_glu_relu_kernel(
             nc.sync.dma_start(raws[c][:], x_rows[:, :, a:b])
 
         nc.scalar.activation(out=warm[:], in_=warm[:], func=RELU)
-        load_x(0)
+        for c in range(len(chunk_cols)):
+            load_x(c)
         nc.sync.dma_start(offsets[:], offs)
-        load_x(1)
-        load_x(2)
         load_scales(nc.sync, w1s, w1_scales)
         load_words(w1w[0], w1_words, 0, 2)
         load_words(w3w[0], w3_words, 0, 2)

@@ -6,7 +6,12 @@ from concourse.masks import make_identity
 K, T, E, C, H, N = 512, 640, 4, 128, 512, 512
 P = 128
 NT = N // P
-WINDOW = 768
+LAST = NT - 1
+LIST_COLS = C // 16
+WINDOW = 2 * 3 * C
+CHUNKS = ((0, 256), (256, 512), (512, T))
+VECTOR_EIGHTHS = 5
+PARTS = ((0, 3), (3, T // P))
 
 FLOPS = 3 * 2 * E * C * K * H
 BYTES = 2 * K * T * 4 + N * T * 4 + 3 * E * (P * 1024 + 16 * 512) + E * C * 4 + P * 64
@@ -49,8 +54,7 @@ def tile_moe_res_glu_relu_kernel(
         w3s = held.tile([P, E, H], U8, name="w3s", align_bytes=64)
         w2s = held.tile([P, E, N], U8, name="w2s", align_bytes=64)
         res = held.tile([P, NT, T], F32, name="res")
-        chunk_cols = [(0, 256), (256, 512), (512, 640)]
-        raws = [held.tile([P, 4, b - a], F32, name=f"raw{a}") for a, b in chunk_cols]
+        raws = [held.tile([P, 4, b - a], F32, name=f"raw{a}") for a, b in CHUNKS]
         windows = [held.tile([P, WINDOW], F32, name=f"window{t}") for t in range(NT)]
 
         nc.gpsimd.memset(scales[:].bitcast(I32), 0)
@@ -61,61 +65,58 @@ def tile_moe_res_glu_relu_kernel(
 
         x_rows = xT.rearrange("(p j) t -> p j t", j=4)
 
-        def load_scales(engine, plane, src):
-            for q in range(4):
-                engine.dma_start(
-                    plane[32 * q : 32 * q + 4, :, :].bitcast(I32),
-                    src[:, 0, 4 * q : 4 * q + 4, :].rearrange("e q i -> q e i").bitcast(I32),
+        def load_scales(tile, src):
+            for g in range(4):
+                nc.sync.dma_start(
+                    tile[32 * g : 32 * g + 4, :, :].bitcast(I32),
+                    src[:, 0, 4 * g : 4 * g + 4, :].rearrange("e q i -> q e i").bitcast(I32),
                 )
 
-        def load_words(tile, src, a, b):
-            nc.sync.dma_start(tile[:].bitcast(I32), src[a:b, 0].rearrange("e p n -> p e n").bitcast(I32))
-
-        def load_x(c):
-            a, b = chunk_cols[c]
-            nc.sync.dma_start(raws[c][:], x_rows[:, :, a:b])
+        def load_words(tile, src, e0, e1):
+            nc.sync.dma_start(tile[:].bitcast(I32), src[e0:e1, 0].rearrange("e p n -> p e n").bitcast(I32))
 
         nc.scalar.activation(out=warm[:], in_=warm[:], func=RELU)
-        for c in range(len(chunk_cols)):
-            load_x(c)
+
+        for raw, (a, b) in zip(raws, CHUNKS):
+            nc.sync.dma_start(raw[:], x_rows[:, :, a:b])
         nc.sync.dma_start(offsets[:], offs)
-        load_scales(nc.sync, w1s, w1_scales)
+        load_scales(w1s, w1_scales)
         load_words(w1w[0], w1_words, 0, 2)
         load_words(w3w[0], w3_words, 0, 2)
-        load_scales(nc.sync, w3s, w3_scales)
+        load_scales(w3s, w3_scales)
         load_words(w1w[1], w1_words, 2, 4)
         load_words(w3w[1], w3_words, 2, 4)
         load_words(w2w, w2_words, 0, E)
-        load_scales(nc.sync, w2s, w2_scales)
+        load_scales(w2s, w2_scales)
         nc.sync.dma_start(gate_t[:], gate[0:P, :])
         nc.sync.dma_start(res[:], xr.rearrange("(t p) c -> p t c", p=P))
 
-        def cast(engine_copy, grouped, g0, raw, r0, width):
-            engine_copy(
-                out=grouped[:, g0 : g0 + width, :].rearrange("p (c i) j -> p c j i", i=4),
-                in_=raw[:, :, r0 : r0 + width].rearrange("p j (c i) -> p c j i", i=4),
+        def round_tokens(copy, grouped, raw, a, b):
+            copy(
+                out=grouped[:, a:b, :].rearrange("p (c i) j -> p c j i", i=4),
+                in_=raw[:, :, a:b].rearrange("p j (c i) -> p c j i", i=4),
             )
 
-        def quantise(grouped, a, b):
+        for raw, (a, b) in zip(raws, CHUNKS):
+            grouped = held.tile([P, b - a, 4], BF16, name=f"grouped{a}", align_bytes=64)
+            share = (b - a) * VECTOR_EIGHTHS // 8
+            round_tokens(nc.vector.tensor_copy, grouped, raw, 0, share)
+            round_tokens(nc.scalar.copy, grouped, raw, share, b - a)
             nc.vector.quantize_mx(
                 out=codes[:, a:b].bitcast(FP8X4),
                 scales=scales[:, a:b],
                 in_=grouped[:].rearrange("p w j -> p (w j)"),
             )
 
-        for raw, (a, b) in zip(raws, chunk_cols):
-            grouped = held.tile([P, b - a, 4], BF16, name=f"grouped{a}", align_bytes=64)
-            share = (b - a) * 5 // 8
-            cast(nc.vector.tensor_copy, grouped, 0, raw, 0, share)
-            cast(nc.scalar.copy, grouped, share, raw, share, b - a - share)
-            quantise(grouped, a, b)
+        def slots_of(e0, e1):
+            return offsets[:, e0 * LIST_COLS : e1 * LIST_COLS]
 
         def gather(e0, e1):
-            lst = offsets[:, e0 * 8 : e1 * 8]
-            nc.vector.tensor_copy(gcodes[:, e0 * C : e1 * C], codes[:].indirect(lst))
-            nc.vector.tensor_copy(gscales[:, e0 * C : e1 * C], scales[:].indirect(lst))
+            nc.vector.tensor_copy(gcodes[:, e0 * C : e1 * C], codes[:].indirect(slots_of(e0, e1)))
+            nc.vector.tensor_copy(gscales[:, e0 * C : e1 * C], scales[:].indirect(slots_of(e0, e1)))
 
-        state = {}
+        hidden = {}
+        hidden_mx = {}
 
         def layer1(e):
             cols = slice(e * C, (e + 1) * C)
@@ -143,14 +144,14 @@ def tile_moe_res_glu_relu_kernel(
                     in1=ra[:, part].rearrange("s (p u d) -> s p u d", u=2, d=2),
                     op=MULT,
                 )
-            state[e] = h
+            hidden[e] = h
 
         def turn(e0, e1, bank):
             n = e1 - e0
             ph = bank[:, 0 : n * 2 * C].rearrange("p (e u c) -> p e u c", e=n, u=2)
             for e in range(e0, e1):
                 for u in range(2):
-                    pairs = state[e][:, u, :, :].rearrange("s p d -> s (p d)").bitcast(F32)
+                    pairs = hidden[e][:, u, :, :].rearrange("s p d -> s (p d)").bitcast(F32)
                     nc.tensor.transpose(ph[:, e - e0, u, :], pairs, ident[:])
             hg = work.tile([P, n, C, 4], BF16, name="hg", align_bytes=64)
             nc.scalar.copy(
@@ -164,19 +165,20 @@ def tile_moe_res_glu_relu_kernel(
             )
             for e in range(e0, e1):
                 cols = slice((e - e0) * C, (e - e0 + 1) * C)
-                state[e] = (hc[:, cols], hs[:, cols])
+                hidden_mx[e] = (hc[:, cols], hs[:, cols])
 
         y0 = held.tile([P, 3, C], F32, name="y0")
         y1 = held.tile([P, 2, C], F32, name="y1")
         y23 = held.tile([P, 2, 2, C], F32, name="y23")
         y_high = held.tile([P, 2, E, C], F32, name="y_high")
 
-        def layer2(e, t0, t1, bank):
-            hc, hs = state[e]
-            py = bank[:, 0 : (t1 - t0) * C].rearrange("p (t c) -> p t c", c=C)
-            for t in range(t0, t1):
+        def layer2(experts, tiles, bank):
+            blocks = [(e, t) for t in tiles for e in experts]
+            py = bank[:, 0 : len(blocks) * C].rearrange("p (b c) -> p b c", c=C)
+            for b, (e, t) in enumerate(blocks):
+                hc, hs = hidden_mx[e]
                 nc.tensor.matmul_mx(
-                    out=py[:, t - t0, :],
+                    out=py[:, b, :],
                     lhsT=w2w[:, e, t * 2 * P : (t + 1) * 2 * P].bitcast(FP4X4),
                     lhsT_scale=w2s[:, e, t * P : (t + 1) * P],
                     rhs=hc.bitcast(FP8X4),
@@ -188,7 +190,7 @@ def tile_moe_res_glu_relu_kernel(
 
         def scatter(t, e0, e1, values):
             nc.vector.tensor_tensor(
-                windows[t][:].indirect(offsets[:, e0 * 8 : e1 * 8]),
+                windows[t][:].indirect(slots_of(e0, e1)),
                 values,
                 gate_t[:, e0 * C : e1 * C],
                 MULT,
@@ -196,9 +198,8 @@ def tile_moe_res_glu_relu_kernel(
 
         def add_by_tensor(t, first, second):
             o = work.tile([P, T], F32, name="o", bufs=NT)
-            parts = ((0, 3), (3, 5))
             turned = []
-            for (b0, b1), bank in zip(parts, first):
+            for (b0, b1), bank in zip(PARTS, first):
                 n = b1 - b0
                 p1 = bank[:, 0 : n * P].rearrange("p (b c) -> p b c", c=P)
                 for b in range(b0, b1):
@@ -211,10 +212,10 @@ def tile_moe_res_glu_relu_kernel(
                         p1[:, b - b0, :], windows[t][:, b * P : (b + 1) * P], ident[:],
                         start=False, stop=(b == b1 - 1), is_transpose=True,
                     )
-                s1 = work.tile([P, n, P], F32, name="s1", bufs=4)
+                s1 = work.tile([P, n, P], F32, name="s1", bufs=2 * len(PARTS))
                 nc.scalar.copy(out=s1[:], in_=p1)
                 turned.append(s1)
-            for (b0, b1), s1, bank in zip(parts, turned, second):
+            for (b0, b1), s1, bank in zip(PARTS, turned, second):
                 n = b1 - b0
                 for b in range(n):
                     nc.tensor.transpose(bank[:, b * P : (b + 1) * P], s1[:, b, :], ident[:])
@@ -224,7 +225,8 @@ def tile_moe_res_glu_relu_kernel(
 
         def add_by_vector(t):
             o = work.tile([P, T], F32, name="o", bufs=NT)
-            for cols, queue in ((slice(0, 384), nc.sync), (slice(384, T), nc.scalar)):
+            for (b0, b1), queue in zip(PARTS, (nc.sync, nc.scalar)):
+                cols = slice(b0 * P, b1 * P)
                 nc.vector.tensor_tensor(out=o[:, cols], in0=windows[t][:, cols], in1=res[:, t, cols], op=ADD)
                 queue.dma_start(out[t * P : (t + 1) * P, cols], o[:, cols])
 
@@ -235,29 +237,29 @@ def tile_moe_res_glu_relu_kernel(
         gather(2, 4)
         turn(0, 1, banks[4])
         layer1(2)
-        nc.scalar.copy(out=y0[:, 0:1, :], in_=layer2(0, 0, 1, banks[6]))
-        py0 = layer2(0, 1, NT, banks[7])
+        nc.scalar.copy(out=y0[:, 0:1, :], in_=layer2([0], [0], banks[6]))
+        py0 = layer2([0], range(1, NT), banks[7])
         nc.scalar.copy(out=y0[:, 1:3, :], in_=py0[:, 0:2, :])
         nc.scalar.copy(out=y_high[:, 1, 0, :], in_=py0[:, 2, :])
         turn(1, 2, banks[5])
         layer1(3)
         turn(2, 4, banks[6])
-        py1 = layer2(1, 0, NT, banks[6])
+        py1 = layer2([1], range(NT), banks[6])
         nc.scalar.copy(out=y1[:], in_=py1[:, 0:2, :])
         nc.scalar.copy(out=y_high[:, :, 1, :], in_=py1[:, 2:4, :])
-        py23 = [layer2(e, 0, NT, bank) for e, bank in ((2, banks[5]), (3, banks[7]))]
-        for e in (2, 3):
-            nc.scalar.copy(out=y23[:, :, e - 2, :], in_=py23[e - 2][:, 0:2, :])
-        for e in (2, 3):
-            nc.scalar.copy(out=y_high[:, :, e, :], in_=py23[e - 2][:, 2:4, :])
-        for t in range(3):
+        for t, bank in ((0, banks[5]), (1, banks[7])):
+            nc.scalar.copy(out=y23[:, t, :, :], in_=layer2([2, 3], [t], bank))
+        for t, bank in ((2, banks[0]), (3, banks[1])):
+            nc.scalar.copy(out=y_high[:, t - 2, 2:E, :], in_=layer2([2, 3], [t], bank))
+        for t in range(LAST):
             scatter(t, 0, 1, y0[:, t, :])
         for t in range(2):
             scatter(t, 1, 2, y1[:, t, :])
-        for t, first, second in ((0, (0, 1), (5, 7)), (1, (2, 3), (0, 1))):
-            scatter(t, 2, E, y23[:, t, :, :].rearrange("p e c -> p (e c)"))
-            add_by_tensor(t, [banks[i] for i in first], [banks[i] for i in second])
+        scatter(0, 2, E, y23[:, 0, :, :].rearrange("p e c -> p (e c)"))
+        add_by_tensor(0, (banks[5], banks[7]), (banks[2], banks[3]))
+        scatter(1, 2, E, y23[:, 1, :, :].rearrange("p e c -> p (e c)"))
+        add_by_tensor(1, (banks[0], banks[1]), (banks[4], banks[6]))
         scatter(2, 1, E, y_high[:, 0, 1:E, :].rearrange("p e c -> p (e c)"))
-        add_by_tensor(2, [banks[4], banks[6]], [banks[2], banks[3]])
-        scatter(3, 0, E, y_high[:, 1, :, :].rearrange("p e c -> p (e c)"))
-        add_by_vector(3)
+        add_by_tensor(2, (banks[5], banks[7]), (banks[2], banks[3]))
+        scatter(LAST, 0, E, y_high[:, 1, :, :].rearrange("p e c -> p (e c)"))
+        add_by_vector(LAST)

@@ -132,17 +132,15 @@ def tile_moe_res_glu_relu_kernel(
                     start=True,
                     stop=True,
                 )
-            ra = work.tile([P, H], F32, name="ra")
+            a_pairs, b_pairs = [acc[:].rearrange("s (p u d) -> s u p d", u=2, d=2) for acc in (pa, pb)]
+            ra = work.tile([P, 2, P, 2], F32, name="ra")
             h = work.tile([P, 2, P, 2], BF16, name="h")
-            step = H // 2 if e == 0 else H
-            for i0 in range(0, H, step):
-                part = slice(i0, i0 + step)
-                nc.scalar.activation(out=ra[:, part], in_=pa[:, part], func=RELU)
+            step = P // 2 if e == 0 else P
+            for p0 in range(0, P, step):
+                ps = slice(p0, p0 + step)
+                nc.scalar.activation(out=ra[:, :, ps, :], in_=a_pairs[:, :, ps, :], func=RELU)
                 nc.vector.tensor_tensor(
-                    out=h[:, :, i0 // 4 : (i0 + step) // 4, :].rearrange("s u p d -> s p u d"),
-                    in0=pb[:, part].rearrange("s (p u d) -> s p u d", u=2, d=2),
-                    in1=ra[:, part].rearrange("s (p u d) -> s p u d", u=2, d=2),
-                    op=MULT,
+                    out=h[:, :, ps, :], in0=b_pairs[:, :, ps, :], in1=ra[:, :, ps, :], op=MULT
                 )
             hidden[e] = h
 

@@ -223,8 +223,8 @@ def tile_moe_res_glu_relu_kernel(
 
         def add_by_vector(t):
             o = work.tile([P, T], F32, name="o", bufs=NT)
-            for (b0, b1), queue in zip(PARTS, (nc.sync, nc.scalar)):
-                cols = slice(b0 * P, b1 * P)
+            for (a, b), queue in zip(CHUNKS, (nc.sync, nc.scalar, nc.sync)):
+                cols = slice(a, b)
                 nc.vector.tensor_tensor(out=o[:, cols], in0=windows[t][:, cols], in1=res[:, t, cols], op=ADD)
                 queue.dma_start(out[t * P : (t + 1) * P, cols], o[:, cols])
 

@@ -219,14 +219,14 @@ def tile_moe_res_glu_relu_kernel(
                     nc.tensor.transpose(bank[:, b * P : (b + 1) * P], s1[:, b, :], ident[:])
                 cols = slice(b0 * P, b1 * P)
                 nc.scalar.copy(out=o[:, cols], in_=bank[:, 0 : n * P])
-                nc.sync.dma_start(out[t * P : (t + 1) * P, cols], o[:, cols])
+                (nc.sync if t < 2 else nc.scalar).dma_start(out[t * P : (t + 1) * P, cols], o[:, cols])
 
         def add_by_vector(t):
             o = work.tile([P, T], F32, name="o", bufs=NT)
-            for (a, b), queue in zip(CHUNKS, (nc.sync, nc.scalar, nc.sync)):
+            for a, b in CHUNKS:
                 cols = slice(a, b)
                 nc.vector.tensor_tensor(out=o[:, cols], in0=windows[t][:, cols], in1=res[:, t, cols], op=ADD)
-                queue.dma_start(out[t * P : (t + 1) * P, cols], o[:, cols])
+                nc.sync.dma_start(out[t * P : (t + 1) * P, cols], o[:, cols])
 
         gather(0, 1)
         layer1(0)
@@ -258,6 +258,6 @@ def tile_moe_res_glu_relu_kernel(
         scatter(1, 2, E, y23[:, 1, :, :].rearrange("p e c -> p (e c)"))
         add_by_tensor(1, (banks[0], banks[1]), (banks[4], banks[6]))
         scatter(2, 1, E, y_high[:, 0, 1:E, :].rearrange("p e c -> p (e c)"))
-        add_by_tensor(2, (banks[5], banks[7]), (banks[2], banks[3]))
+        add_by_tensor(2, (banks[0], banks[1]), (banks[5], banks[7]))
         scatter(LAST, 0, E, y_high[:, 1, :, :].rearrange("p e c -> p (e c)"))
         add_by_vector(LAST)

@@ -49,16 +49,20 @@ def tile_moe_res_glu_relu_kernel(
         gscales = held.tile([P, E * C], U8, name="gscales", align_bytes=64)
         w1w = [held.tile([P, 2, 2 * H], U8, name=f"w1w{g}", align_bytes=64) for g in range(2)]
         w3w = [held.tile([P, 2, 2 * H], U8, name=f"w3w{g}", align_bytes=64) for g in range(2)]
-        w2w = held.tile([P, E, 2 * N], U8, name="w2w", align_bytes=64)
+        w2w = held.tile([P, E + 1, 2 * N], U8, name="w2w", align_bytes=64)
         w1s = held.tile([P, E, H], U8, name="w1s", align_bytes=64)
         w3s = held.tile([P, E, H], U8, name="w3s", align_bytes=64)
-        w2s = held.tile([P, E, N], U8, name="w2s", align_bytes=64)
+        w2s = held.tile([P, E + 1, N], U8, name="w2s", align_bytes=64)
         res = held.tile([P, NT, T], F32, name="res")
-        raws = [held.tile([P, 4, b - a], F32, name=f"raw{a}") for a, b in CHUNKS]
+        raws = [held.tile([P, 4, b - a], F32, name=f"raw{a}", align_bytes=64) for a, b in CHUNKS]
         windows = [held.tile([P, WINDOW], F32, name=f"window{t}") for t in range(NT)]
 
         nc.gpsimd.memset(scales[:].bitcast(I32), 0)
         make_identity(nc, ident[:])
+        hc_all = held.tile([P, E * C], U32, name="hc_all", align_bytes=64)
+        nc.gpsimd.memset(w2w[:, E, 0 : 2 * P].bitcast(I32), 0)
+        nc.gpsimd.memset(w2s[:, E, 0:P].bitcast(I32), 0)
+        nc.gpsimd.memset(hc_all[:].bitcast(I32), 0)
         nc.vector.memset(warm[:], 0.0)
         for t in range(NT):
             nc.vector.memset(windows[t][:, 0:T], 0.0)
@@ -68,12 +72,12 @@ def tile_moe_res_glu_relu_kernel(
         def load_scales(tile, src):
             for g in range(4):
                 nc.sync.dma_start(
-                    tile[32 * g : 32 * g + 4, :, :].bitcast(I32),
+                    tile[32 * g : 32 * g + 4, 0:E, :].bitcast(I32),
                     src[:, 0, 4 * g : 4 * g + 4, :].rearrange("e q i -> q e i").bitcast(I32),
                 )
 
         def load_words(tile, src, e0, e1):
-            nc.sync.dma_start(tile[:].bitcast(I32), src[e0:e1, 0].rearrange("e p n -> p e n").bitcast(I32))
+            nc.sync.dma_start(tile[:, 0 : e1 - e0, :].bitcast(I32), src[e0:e1, 0].rearrange("e p n -> p e n").bitcast(I32))
 
         nc.scalar.activation(out=warm[:], in_=warm[:], func=RELU)
 
@@ -102,6 +106,19 @@ def tile_moe_res_glu_relu_kernel(
             share = (b - a) * VECTOR_EIGHTHS // 8
             round_tokens(nc.vector.tensor_copy, grouped, raw, 0, share)
             round_tokens(nc.scalar.copy, grouped, raw, share, b - a)
+            if a == 0:
+                hs_all = held.tile([P, E * C], U8, name="raw0", align_bytes=64)
+                nc.vector.memset(hs_all[:].bitcast(I32), 0)
+                for i in range(3):
+                    nc.tensor.matmul_mx(
+                        out=banks[5 + i][:],
+                        lhsT=w2w[:, E, 0 : 2 * P].bitcast(FP4X4),
+                        lhsT_scale=w2s[:, E, 0:P],
+                        rhs=hc_all[:].bitcast(FP8X4),
+                        rhs_scale=hs_all[:],
+                        start=True,
+                        stop=True,
+                    )
             nc.vector.quantize_mx(
                 out=codes[:, a:b].bitcast(FP8X4),
                 scales=scales[:, a:b],
@@ -156,10 +173,10 @@ def tile_moe_res_glu_relu_kernel(
                 out=hg[:].rearrange("p e c j -> p (e c j)").bitcast(F32).rearrange("p (e c u) -> p e c u", e=n, u=2),
                 in_=ph.rearrange("p e u c -> p e c u"),
             )
-            hc = work.tile([P, n * C], U32, name="hc", align_bytes=64)
-            hs = work.tile([P, n * C], U8, name="hs", align_bytes=64)
+            hc = hc_all[:, e0 * C : e1 * C]
+            hs = hs_all[:, e0 * C : e1 * C]
             nc.vector.quantize_mx(
-                out=hc[:].bitcast(FP8X4), scales=hs[:], in_=hg[:].rearrange("p e c j -> p (e c j)")
+                out=hc.bitcast(FP8X4), scales=hs, in_=hg[:].rearrange("p e c j -> p (e c j)")
             )
             for e in range(e0, e1):
                 cols = slice((e - e0) * C, (e - e0 + 1) * C)

@@ -7,6 +7,7 @@ K, T, E, C, H, N = 512, 640, 4, 128, 512, 512
 P = 128
 NT = N // P
 LAST = NT - 1
+LAST_E = E - 1
 LIST_COLS = C // 16
 WINDOW = 2 * 3 * C
 CHUNKS = ((0, 256), (256, 512), (512, T))
@@ -45,7 +46,7 @@ def tile_moe_res_glu_relu_kernel(
         warm = held.tile([P, 1], F32, name="warm")
         codes = held.tile([P, T], U32, name="codes", align_bytes=64)
         scales = held.tile([P, T], U8, name="scales", align_bytes=64)
-        gcodes = held.tile([P, E * C], U32, name="gcodes", align_bytes=64)
+        gcodes = held.tile([P, LAST_E * C], U32, name="gcodes", align_bytes=64)
         gscales = held.tile([P, E * C], U8, name="gscales", align_bytes=64)
         w1w = [held.tile([P, 2, 2 * H], U8, name=f"w1w{g}", align_bytes=64) for g in range(2)]
         w3w = [held.tile([P, 2, 2 * H], U8, name=f"w3w{g}", align_bytes=64) for g in range(2)]
@@ -106,8 +107,13 @@ def tile_moe_res_glu_relu_kernel(
             share = (b - a) * VECTOR_EIGHTHS // 8
             round_tokens(nc.vector.tensor_copy, grouped, raw, 0, share)
             round_tokens(nc.scalar.copy, grouped, raw, share, b - a)
+            nc.vector.quantize_mx(
+                out=codes[:, a:b].bitcast(FP8X4),
+                scales=scales[:, a:b],
+                in_=grouped[:].rearrange("p w j -> p (w j)"),
+            )
             if a == 0:
-                hs_all = held.tile([P, E * C], U8, name="raw0", align_bytes=64)
+                hs_all = held.tile([P, E * C], U8, name="grouped0", align_bytes=64)
                 nc.vector.memset(hs_all[:].bitcast(I32), 0)
                 for i in range(3):
                     nc.tensor.matmul_mx(
@@ -119,45 +125,45 @@ def tile_moe_res_glu_relu_kernel(
                         start=True,
                         stop=True,
                     )
-            nc.vector.quantize_mx(
-                out=codes[:, a:b].bitcast(FP8X4),
-                scales=scales[:, a:b],
-                in_=grouped[:].rearrange("p w j -> p (w j)"),
-            )
 
         def slots_of(e0, e1):
             return offsets[:, e0 * LIST_COLS : e1 * LIST_COLS]
 
-        def gather(e0, e1):
-            nc.vector.tensor_copy(gcodes[:, e0 * C : e1 * C], codes[:].indirect(slots_of(e0, e1)))
+        token_words = {}
+
+        def gather_words(e, words):
+            nc.vector.tensor_copy(words, codes[:].indirect(slots_of(e, e + 1)))
+            token_words[e] = words
+
+        def gather_scales(e0, e1):
             nc.vector.tensor_copy(gscales[:, e0 * C : e1 * C], scales[:].indirect(slots_of(e0, e1)))
 
         hidden = {}
         hidden_mx = {}
 
-        def layer1(e):
-            cols = slice(e * C, (e + 1) * C)
-            pa = banks[2 * (e % 2)]
-            pb = banks[2 * (e % 2) + 1]
+        def layer1(e, pa, pb):
             for acc, words, sc in ((pa, w1w, w1s), (pb, w3w, w3s)):
                 nc.tensor.matmul_mx(
                     out=acc[:],
-                    lhsT=gcodes[:, cols].bitcast(FP8X4),
-                    lhsT_scale=gscales[:, cols],
+                    lhsT=token_words[e].bitcast(FP8X4),
+                    lhsT_scale=gscales[:, e * C : (e + 1) * C],
                     rhs=words[e // 2][:, e % 2, :].bitcast(FP4X4),
                     rhs_scale=sc[:, e, :],
                     start=True,
                     stop=True,
                 )
             a_pairs, b_pairs = [acc[:].rearrange("s (p u d) -> s u p d", u=2, d=2) for acc in (pa, pb)]
-            ra = work.tile([P, 2, P, 2], F32, name="ra")
-            h = work.tile([P, 2, P, 2], BF16, name="h")
+            h = work.tile([P, 2, P, 2], BF16, name="h", bufs=4)
             step = P // 2 if e == 0 else P
             for p0 in range(0, P, step):
                 ps = slice(p0, p0 + step)
-                nc.scalar.activation(out=ra[:, :, ps, :], in_=a_pairs[:, :, ps, :], func=RELU)
+                if e == 0:
+                    ra = held.tile([P, 2, step, 2], F32, name=f"ra_half{p0 // step}", align_bytes=64)
+                else:
+                    ra = work.tile([P, 2, step, 2], F32, name="ra", bufs=2)
+                nc.scalar.activation(out=ra[:], in_=a_pairs[:, :, ps, :], func=RELU)
                 nc.vector.tensor_tensor(
-                    out=h[:, :, ps, :], in0=b_pairs[:, :, ps, :], in1=ra[:, :, ps, :], op=MULT
+                    out=h[:, :, ps, :], in0=b_pairs[:, :, ps, :], in1=ra[:], op=MULT
                 )
             hidden[e] = h
 
@@ -245,21 +251,24 @@ def tile_moe_res_glu_relu_kernel(
                 nc.vector.tensor_tensor(out=o[:, cols], in0=windows[t][:, cols], in1=res[:, t, cols], op=ADD)
                 nc.sync.dma_start(out[t * P : (t + 1) * P, cols], o[:, cols])
 
-        gather(0, 1)
-        layer1(0)
-        gather(1, 2)
-        layer1(1)
-        gather(2, 4)
-        turn(0, 1, banks[4])
-        layer1(2)
-        nc.scalar.copy(out=y0[:, 0:1, :], in_=layer2([0], [0], banks[6]))
-        py0 = layer2([0], range(1, NT), banks[7])
+        for e in range(LAST_E):
+            gather_words(e, gcodes[:, e * C : (e + 1) * C])
+            gather_scales(e, e + 1 if e + 1 < LAST_E else E)
+        layer1(0, banks[0], banks[1])
+        last_words = held.tile([P, C], U32, name="ra_half0", align_bytes=64)
+        gather_words(LAST_E, last_words[:])
+        layer1(1, banks[2], banks[3])
+
+        turn(0, 1, banks[7])
+        layer1(2, banks[4], banks[5])
+        nc.scalar.copy(out=y0[:, 0:1, :], in_=layer2([0], [0], banks[4]))
+        py0 = layer2([0], range(1, NT), banks[1])
         nc.scalar.copy(out=y0[:, 1:3, :], in_=py0[:, 0:2, :])
         nc.scalar.copy(out=y_high[:, 1, 0, :], in_=py0[:, 2, :])
-        turn(1, 2, banks[5])
-        layer1(3)
-        turn(2, 4, banks[6])
-        py1 = layer2([1], range(NT), banks[6])
+        turn(1, 2, banks[2])
+        layer1(3, banks[0], banks[6])
+        turn(2, 4, banks[4])
+        py1 = layer2([1], range(NT), banks[4])
         nc.scalar.copy(out=y1[:], in_=py1[:, 0:2, :])
         nc.scalar.copy(out=y_high[:, :, 1, :], in_=py1[:, 2:4, :])
         for t, bank in ((0, banks[5]), (1, banks[7])):

@@ -12,7 +12,7 @@ LIST_COLS = C // 16
 WINDOW = 2 * 3 * C
 CHUNKS = ((0, 256), (256, 512), (512, T))
 VECTOR_EIGHTHS = 5
-PARTS = ((0, 3), (3, T // P))
+PARTS = ((0, 1), (1, 3), (3, 5))
 
 FLOPS = 3 * 2 * E * C * K * H
 BYTES = 2 * K * T * 4 + N * T * 4 + 3 * E * (P * 1024 + 16 * 512) + E * C * 4 + P * 64
@@ -242,7 +242,8 @@ def tile_moe_res_glu_relu_kernel(
                     nc.tensor.transpose(bank[:, b * P : (b + 1) * P], s1[:, b, :], ident[:])
                 cols = slice(b0 * P, b1 * P)
                 nc.scalar.copy(out=o[:, cols], in_=bank[:, 0 : n * P])
-                (nc.sync if t < 2 else nc.scalar).dma_start(out[t * P : (t + 1) * P, cols], o[:, cols])
+                if b1 == T // P:
+                    (nc.sync if t < 2 else nc.scalar).dma_start(out[t * P : (t + 1) * P, :], o[:])
 
         def add_by_vector(t):
             o = work.tile([P, T], F32, name="o", bufs=NT)
@@ -280,10 +281,10 @@ def tile_moe_res_glu_relu_kernel(
         for t in range(2):
             scatter(t, 1, 2, y1[:, t, :])
         scatter(0, 2, E, y23[:, 0, :, :].rearrange("p e c -> p (e c)"))
-        add_by_tensor(0, (banks[5], banks[7]), (banks[2], banks[3]))
+        add_by_tensor(0, (banks[5], banks[7], banks[2]), (banks[5], banks[7], banks[2]))
         scatter(1, 2, E, y23[:, 1, :, :].rearrange("p e c -> p (e c)"))
-        add_by_tensor(1, (banks[0], banks[1]), (banks[4], banks[6]))
+        add_by_tensor(1, (banks[0], banks[1], banks[3]), (banks[0], banks[1], banks[3]))
         scatter(2, 1, E, y_high[:, 0, 1:E, :].rearrange("p e c -> p (e c)"))
-        add_by_tensor(2, (banks[0], banks[1]), (banks[5], banks[7]))
+        add_by_tensor(2, (banks[4], banks[6], banks[5]), (banks[4], banks[6], banks[5]))
         scatter(LAST, 0, E, y_high[:, 1, :, :].rearrange("p e c -> p (e c)"))
         add_by_vector(LAST)

@@ -14,6 +14,8 @@ CHUNKS = ((0, 256), (256, 512), (512, T))
 VECTOR_EIGHTHS = 5
 PARTS = ((0, 1), (1, 3), (3, 5))
 
+LAST_PARTS = ((0, 128), (128, 384), (384, T))
+
 FLOPS = 3 * 2 * E * C * K * H
 BYTES = 2 * K * T * 4 + N * T * 4 + 3 * E * (P * 1024 + 16 * 512) + E * C * 4 + P * 64
 
@@ -46,8 +48,6 @@ def tile_moe_res_glu_relu_kernel(
         warm = held.tile([P, 1], F32, name="warm")
         codes = held.tile([P, T], U32, name="codes", align_bytes=64)
         scales = held.tile([P, T], U8, name="scales", align_bytes=64)
-        gcodes = held.tile([P, LAST_E * C], U32, name="gcodes", align_bytes=64)
-        gscales = held.tile([P, E * C], U8, name="gscales", align_bytes=64)
         w1w = [held.tile([P, 2, 2 * H], U8, name=f"w1w{g}", align_bytes=64) for g in range(2)]
         w3w = [held.tile([P, 2, 2 * H], U8, name=f"w3w{g}", align_bytes=64) for g in range(2)]
         w2w = held.tile([P, E + 1, 2 * N], U8, name="w2w", align_bytes=64)
@@ -131,40 +131,45 @@ def tile_moe_res_glu_relu_kernel(
 
         token_words = {}
 
-        def gather_words(e, words):
-            nc.vector.tensor_copy(words, codes[:].indirect(slots_of(e, e + 1)))
-            token_words[e] = words
+        token_scales = {}
 
-        def gather_scales(e0, e1):
-            nc.vector.tensor_copy(gscales[:, e0 * C : e1 * C], scales[:].indirect(slots_of(e0, e1)))
+        def gather_words(e0, e1, buffer):
+            words = held.tile([P, (e1 - e0) * C], U32, name=buffer, align_bytes=64)
+            nc.vector.tensor_copy(words[:], codes[:].indirect(slots_of(e0, e1)))
+            for e in range(e0, e1):
+                token_words[e] = words[:, (e - e0) * C : (e - e0 + 1) * C]
+
+        def gather_scales(e0, e1, buffer):
+            planes = held.tile([P, (e1 - e0) * C], U8, name=buffer, align_bytes=64)
+            nc.vector.tensor_copy(planes[:], scales[:].indirect(slots_of(e0, e1)))
+            for e in range(e0, e1):
+                token_scales[e] = planes[:, (e - e0) * C : (e - e0 + 1) * C]
 
         hidden = {}
         hidden_mx = {}
 
         def layer1(e, pa, pb):
+            multiply1(e, pa, pb)
+            gate_units(e, pa, pb)
+
+        def multiply1(e, pa, pb):
             for acc, words, sc in ((pa, w1w, w1s), (pb, w3w, w3s)):
                 nc.tensor.matmul_mx(
                     out=acc[:],
                     lhsT=token_words[e].bitcast(FP8X4),
-                    lhsT_scale=gscales[:, e * C : (e + 1) * C],
+                    lhsT_scale=token_scales[e],
                     rhs=words[e // 2][:, e % 2, :].bitcast(FP4X4),
                     rhs_scale=sc[:, e, :],
                     start=True,
                     stop=True,
                 )
+
+        def gate_units(e, pa, pb):
             a_pairs, b_pairs = [acc[:].rearrange("s (p u d) -> s u p d", u=2, d=2) for acc in (pa, pb)]
-            h = work.tile([P, 2, P, 2], BF16, name="h", bufs=4)
-            step = P // 2 if e == 0 else P
-            for p0 in range(0, P, step):
-                ps = slice(p0, p0 + step)
-                if e == 0:
-                    ra = held.tile([P, 2, step, 2], F32, name=f"ra_half{p0 // step}", align_bytes=64)
-                else:
-                    ra = work.tile([P, 2, step, 2], F32, name="ra", bufs=2)
-                nc.scalar.activation(out=ra[:], in_=a_pairs[:, :, ps, :], func=RELU)
-                nc.vector.tensor_tensor(
-                    out=h[:, :, ps, :], in0=b_pairs[:, :, ps, :], in1=ra[:], op=MULT
-                )
+            h = held.tile([P, 2, P, 2], BF16, name="words1" if e == 2 else f"h{e}", align_bytes=64)
+            ra = work.tile([P, 2, P, 2], F32, name="ra", bufs=3)
+            nc.scalar.activation(out=ra[:], in_=a_pairs, func=RELU)
+            nc.vector.tensor_tensor(out=h[:], in0=b_pairs, in1=ra[:], op=MULT)
             hidden[e] = h
 
         def turn(e0, e1, bank):
@@ -247,27 +252,31 @@ def tile_moe_res_glu_relu_kernel(
 
         def add_by_vector(t):
             o = work.tile([P, T], F32, name="o", bufs=NT)
-            for a, b in CHUNKS:
+            for a, b in LAST_PARTS:
                 cols = slice(a, b)
                 nc.vector.tensor_tensor(out=o[:, cols], in0=windows[t][:, cols], in1=res[:, t, cols], op=ADD)
                 nc.sync.dma_start(out[t * P : (t + 1) * P, cols], o[:, cols])
 
-        for e in range(LAST_E):
-            gather_words(e, gcodes[:, e * C : (e + 1) * C])
-            gather_scales(e, e + 1 if e + 1 < LAST_E else E)
+        gather_words(0, 1, "words0")
+        gather_scales(0, 1, "planes0")
+        gather_words(1, 2, "words1")
+        gather_scales(1, 2, "planes1")
+        gather_words(2, 3, "words2")
+        gather_scales(2, E, "planes2")
         layer1(0, banks[0], banks[1])
-        last_words = held.tile([P, C], U32, name="ra_half0", align_bytes=64)
-        gather_words(LAST_E, last_words[:])
-        layer1(1, banks[2], banks[3])
-
+        multiply1(1, banks[2], banks[3])
+        gather_words(LAST_E, E, "words1")
+        gate_units(1, banks[2], banks[3])
         turn(0, 1, banks[7])
-        layer1(2, banks[4], banks[5])
+        multiply1(2, banks[4], banks[5])
+        multiply1(3, banks[0], banks[6])
+        gate_units(2, banks[4], banks[5])
         nc.scalar.copy(out=y0[:, 0:1, :], in_=layer2([0], [0], banks[4]))
         py0 = layer2([0], range(1, NT), banks[1])
         nc.scalar.copy(out=y0[:, 1:3, :], in_=py0[:, 0:2, :])
         nc.scalar.copy(out=y_high[:, 1, 0, :], in_=py0[:, 2, :])
         turn(1, 2, banks[2])
-        layer1(3, banks[0], banks[6])
+        gate_units(3, banks[0], banks[6])
         turn(2, 4, banks[4])
         py1 = layer2([1], range(NT), banks[4])
         nc.scalar.copy(out=y1[:], in_=py1[:, 0:2, :])

@@ -12,7 +12,6 @@ LIST_COLS = C // 16
 WINDOW = 2 * 3 * C
 CHUNKS = ((0, 256), (256, 512), (512, T))
 VECTOR_EIGHTHS = 5
-PARTS = ((0, 1), (1, 3), (3, 5))
 
 LAST_PARTS = ((0, 128), (128, 384), (384, T))
 
@@ -30,6 +29,7 @@ FP4X4 = mybir.dt.float4_e2m1fn_x4
 ADD = mybir.AluOpType.add
 MULT = mybir.AluOpType.mult
 RELU = mybir.ActivationFunctionType.Relu
+COPY = mybir.ActivationFunctionType.Copy
 
 
 def tile_moe_res_glu_relu_kernel(
@@ -195,8 +195,9 @@ def tile_moe_res_glu_relu_kernel(
 
         y0 = held.tile([P, 3, C], F32, name="y0")
         y1 = held.tile([P, 2, C], F32, name="y1")
-        y23 = held.tile([P, 2, 2, C], F32, name="y23")
-        y_high = held.tile([P, 2, E, C], F32, name="y_high")
+        y23 = held.tile([P, 2, C], F32, name="y23")
+        gate_cols = held.tile([P, E, 1], F32, name="gate_cols")
+        by_slot = {}
 
         def layer2(experts, tiles, bank):
             blocks = [(e, t) for t in tiles for e in experts]
@@ -214,6 +215,40 @@ def tile_moe_res_glu_relu_kernel(
                 )
             return py
 
+        def turn_gate(bank):
+            turned_gate = bank[:].rearrange("p (e c) -> p e c", e=E)
+            for e in range(E):
+                nc.tensor.transpose(turned_gate[:, e, :], gate_t[:, e * C : (e + 1) * C], ident[:])
+            nc.scalar.copy(out=gate_cols[:], in_=turned_gate[:, :, 0:1])
+
+        def layer2_by_slot(e, t0, bank_cols):
+            hc, hs = hidden_mx[e]
+            for t in range(t0, NT):
+                nc.tensor.matmul_mx(
+                    out=bank_cols[:, (t - t0) * P : (t - t0 + 1) * P],
+                    lhsT=hc.bitcast(FP8X4),
+                    lhsT_scale=hs,
+                    rhs=w2w[:, e, t * 2 * P : (t + 1) * 2 * P].bitcast(FP4X4),
+                    rhs_scale=w2s[:, e, t * P : (t + 1) * P],
+                    start=True,
+                    stop=True,
+                )
+            gated = held.tile([P, (NT - t0) * P], F32, name=f"gated{e}")
+            nc.scalar.activation(out=gated[:], in_=bank_cols, func=COPY, scale=gate_cols[:, e, :])
+            for t in range(t0, NT):
+                by_slot[e, t] = gated[:, (t - t0) * P : (t - t0 + 1) * P]
+
+        def turn_gated(t, e0, bank):
+            cols = bank[:, 0 : (E - e0) * C]
+            for e in range(e0, E):
+                nc.tensor.transpose(cols[:, (e - e0) * C : (e - e0 + 1) * C], by_slot[e, t], ident[:])
+            values = held.tile([P, (E - e0) * C], F32, name=f"values{t}")
+            nc.scalar.copy(out=values[:], in_=cols)
+            return values
+
+        def scatter_gated(t, e0, values):
+            nc.vector.tensor_copy(windows[t][:].indirect(slots_of(e0, E)), values[:])
+
         def scatter(t, e0, e1, values):
             nc.vector.tensor_tensor(
                 windows[t][:].indirect(slots_of(e0, e1)),
@@ -222,36 +257,13 @@ def tile_moe_res_glu_relu_kernel(
                 MULT,
             )
 
-        def add_by_tensor(t, first, second):
-            o = work.tile([P, T], F32, name="o", bufs=NT)
-            turned = []
-            for (b0, b1), bank in zip(PARTS, first):
-                n = b1 - b0
-                p1 = bank[:, 0 : n * P].rearrange("p (b c) -> p b c", c=P)
-                for b in range(b0, b1):
-                    nc.tensor.matmul(
-                        p1[:, b - b0, :], res[:, t, b * P : (b + 1) * P], ident[:],
-                        start=(b == b0), stop=False, is_transpose=True,
-                    )
-                for b in range(b0, b1):
-                    nc.tensor.matmul(
-                        p1[:, b - b0, :], windows[t][:, b * P : (b + 1) * P], ident[:],
-                        start=False, stop=(b == b1 - 1), is_transpose=True,
-                    )
-                s1 = work.tile([P, n, P], F32, name="s1", bufs=2 * len(PARTS))
-                nc.scalar.copy(out=s1[:], in_=p1)
-                turned.append(s1)
-            for (b0, b1), s1, bank in zip(PARTS, turned, second):
-                n = b1 - b0
-                for b in range(n):
-                    nc.tensor.transpose(bank[:, b * P : (b + 1) * P], s1[:, b, :], ident[:])
-                cols = slice(b0 * P, b1 * P)
-                nc.scalar.copy(out=o[:, cols], in_=bank[:, 0 : n * P])
-                if b1 == T // P:
-                    (nc.sync if t < 2 else nc.scalar).dma_start(out[t * P : (t + 1) * P, :], o[:])
+        def add_by_gpsimd(t):
+            o = held.tile([P, T], F32, name=f"gated{t}")
+            nc.gpsimd.tensor_tensor(out=o[:], in0=windows[t][:, 0:T], in1=res[:, t, :], op=ADD)
+            nc.scalar.dma_start(out[t * P : (t + 1) * P, :], o[:])
 
         def add_by_vector(t):
-            o = work.tile([P, T], F32, name="o", bufs=NT)
+            o = held.tile([P, T], F32, name=f"sum{t}")
             for a, b in LAST_PARTS:
                 cols = slice(a, b)
                 nc.vector.tensor_tensor(out=o[:, cols], in0=windows[t][:, cols], in1=res[:, t, cols], op=ADD)
@@ -272,28 +284,26 @@ def tile_moe_res_glu_relu_kernel(
         multiply1(3, banks[0], banks[6])
         gate_units(2, banks[4], banks[5])
         nc.scalar.copy(out=y0[:, 0:1, :], in_=layer2([0], [0], banks[4]))
-        py0 = layer2([0], range(1, NT), banks[1])
-        nc.scalar.copy(out=y0[:, 1:3, :], in_=py0[:, 0:2, :])
-        nc.scalar.copy(out=y_high[:, 1, 0, :], in_=py0[:, 2, :])
+        nc.scalar.copy(out=y0[:, 1:3, :], in_=layer2([0], [1, 2], banks[1]))
         turn(1, 2, banks[2])
         gate_units(3, banks[0], banks[6])
         turn(2, 4, banks[4])
-        py1 = layer2([1], range(NT), banks[4])
-        nc.scalar.copy(out=y1[:], in_=py1[:, 0:2, :])
-        nc.scalar.copy(out=y_high[:, :, 1, :], in_=py1[:, 2:4, :])
-        for t, bank in ((0, banks[5]), (1, banks[7])):
-            nc.scalar.copy(out=y23[:, t, :, :], in_=layer2([2, 3], [t], bank))
-        for t, bank in ((2, banks[0]), (3, banks[1])):
-            nc.scalar.copy(out=y_high[:, t - 2, 2:E, :], in_=layer2([2, 3], [t], bank))
+        nc.scalar.copy(out=y1[:], in_=layer2([1], range(2), banks[4]))
+        turn_gate(banks[1])
+        nc.scalar.copy(out=y23[:], in_=layer2([2, 3], [0], banks[5]))
+        layer2_by_slot(2, 1, banks[7][:, 0 : 3 * P])
+        layer2_by_slot(3, 1, banks[0][:, 0 : 3 * P])
+        values1 = turn_gated(1, 2, banks[2])
+        layer2_by_slot(1, 2, banks[4][:, 0 : 2 * P])
+        values2 = turn_gated(2, 1, banks[3])
+        layer2_by_slot(0, 3, banks[5][:, 0:P])
+        values3 = turn_gated(3, 0, banks[6])
         for t in range(LAST):
             scatter(t, 0, 1, y0[:, t, :])
         for t in range(2):
             scatter(t, 1, 2, y1[:, t, :])
-        scatter(0, 2, E, y23[:, 0, :, :].rearrange("p e c -> p (e c)"))
-        add_by_tensor(0, (banks[5], banks[7], banks[2]), (banks[5], banks[7], banks[2]))
-        scatter(1, 2, E, y23[:, 1, :, :].rearrange("p e c -> p (e c)"))
-        add_by_tensor(1, (banks[0], banks[1], banks[3]), (banks[0], banks[1], banks[3]))
-        scatter(2, 1, E, y_high[:, 0, 1:E, :].rearrange("p e c -> p (e c)"))
-        add_by_tensor(2, (banks[4], banks[6], banks[5]), (banks[4], banks[6], banks[5]))
-        scatter(LAST, 0, E, y_high[:, 1, :, :].rearrange("p e c -> p (e c)"))
+        scatter(0, 2, E, y23[:].rearrange("p e c -> p (e c)"))
+        for t, values in enumerate((values1, values2, values3)):
+            add_by_gpsimd(t)
+            scatter_gated(t + 1, 2 - t, values)
         add_by_vector(LAST)

@@ -194,7 +194,7 @@ def tile_moe_res_glu_relu_kernel(
                 hidden_mx[e] = (hc[:, cols], hs[:, cols])
 
         y0 = held.tile([P, 3, C], F32, name="y0")
-        y1 = held.tile([P, 2, C], F32, name="y1")
+        y1 = held.tile([P, 3, C], F32, name="y1")
         y23 = held.tile([P, 2, C], F32, name="y23")
         gate_cols = held.tile([P, E, 1], F32, name="gate_cols")
         by_slot = {}
@@ -288,22 +288,22 @@ def tile_moe_res_glu_relu_kernel(
         turn(1, 2, banks[2])
         gate_units(3, banks[0], banks[6])
         turn(2, 4, banks[4])
-        nc.scalar.copy(out=y1[:], in_=layer2([1], range(2), banks[4]))
+        nc.scalar.copy(out=y1[:], in_=layer2([1], range(3), banks[4]))
         turn_gate(banks[1])
         nc.scalar.copy(out=y23[:], in_=layer2([2, 3], [0], banks[5]))
         layer2_by_slot(2, 1, banks[7][:, 0 : 3 * P])
         layer2_by_slot(3, 1, banks[0][:, 0 : 3 * P])
         values1 = turn_gated(1, 2, banks[2])
-        layer2_by_slot(1, 2, banks[4][:, 0 : 2 * P])
-        values2 = turn_gated(2, 1, banks[3])
+        values2 = turn_gated(2, 2, banks[3])
+        layer2_by_slot(1, 3, banks[4][:, 0:P])
         layer2_by_slot(0, 3, banks[5][:, 0:P])
         values3 = turn_gated(3, 0, banks[6])
         for t in range(LAST):
             scatter(t, 0, 1, y0[:, t, :])
-        for t in range(2):
+        for t in range(LAST):
             scatter(t, 1, 2, y1[:, t, :])
         scatter(0, 2, E, y23[:].rearrange("p e c -> p (e c)"))
-        for t, values in enumerate((values1, values2, values3)):
+        for t, (e0, values) in enumerate(((2, values1), (2, values2), (0, values3))):
             add_by_gpsimd(t)
-            scatter_gated(t + 1, 2 - t, values)
+            scatter_gated(t + 1, e0, values)
         add_by_vector(LAST)

@@ -6,13 +6,9 @@ from concourse.masks import make_identity
 K, T, E, C, H, N = 512, 640, 4, 128, 512, 512
 P = 128
 NT = N // P
-LAST = NT - 1
-LAST_E = E - 1
 LIST_COLS = C // 16
-WINDOW = 2 * 3 * C
 CHUNKS = ((0, 256), (256, 512), (512, T))
 VECTOR_EIGHTHS = 5
-
 LAST_PARTS = ((0, 128), (128, 384), (384, T))
 
 FLOPS = 3 * 2 * E * C * K * H
@@ -38,47 +34,43 @@ def tile_moe_res_glu_relu_kernel(
     nc = tc.nc
     with ExitStack() as ctx:
         held = ctx.enter_context(tc.tile_pool(name="held", bufs=1))
-        work = ctx.enter_context(tc.tile_pool(name="work", bufs=2))
         psum = ctx.enter_context(tc.psum_pool(name="psum", bufs=1))
         banks = [psum.tile([P, 512], F32, name=f"bank{i}") for i in range(8)]
 
         offsets = held.tile([P, E * C // 16], U16, name="offsets")
-        gate_t = held.tile([P, E * C], F32, name="gate_t")
+        gates = [held.tile([P, 2 * C], F32, name=f"gate{g}") for g in range(2)]
         ident = held.tile([P, P], F32, name="ident")
         warm = held.tile([P, 1], F32, name="warm")
         codes = held.tile([P, T], U32, name="codes", align_bytes=64)
         scales = held.tile([P, T], U8, name="scales", align_bytes=64)
         w1w = [held.tile([P, 2, 2 * H], U8, name=f"w1w{g}", align_bytes=64) for g in range(2)]
         w3w = [held.tile([P, 2, 2 * H], U8, name=f"w3w{g}", align_bytes=64) for g in range(2)]
-        w2w = held.tile([P, E + 1, 2 * N], U8, name="w2w", align_bytes=64)
+        w2w = [held.tile([P, 2, 2 * N], U8, name=f"w2w{g}", align_bytes=64) for g in range(2)]
         w1s = held.tile([P, E, H], U8, name="w1s", align_bytes=64)
         w3s = held.tile([P, E, H], U8, name="w3s", align_bytes=64)
-        w2s = held.tile([P, E + 1, N], U8, name="w2s", align_bytes=64)
+        w2s = held.tile([P, E, N], U8, name="w2s", align_bytes=64)
         res = held.tile([P, NT, T], F32, name="res")
         raws = [held.tile([P, 4, b - a], F32, name=f"raw{a}", align_bytes=64) for a, b in CHUNKS]
-        windows = [held.tile([P, WINDOW], F32, name=f"window{t}") for t in range(NT)]
+        windows = [held.tile([P, T], F32, name=f"window{t}") for t in range(NT)]
+        values = held.tile([P, NT * E * C], F32, name="values", align_bytes=64)
 
         nc.gpsimd.memset(scales[:].bitcast(I32), 0)
         make_identity(nc, ident[:])
-        hc_all = held.tile([P, E * C], U32, name="hc_all", align_bytes=64)
-        nc.gpsimd.memset(w2w[:, E, 0 : 2 * P].bitcast(I32), 0)
-        nc.gpsimd.memset(w2s[:, E, 0:P].bitcast(I32), 0)
-        nc.gpsimd.memset(hc_all[:].bitcast(I32), 0)
         nc.vector.memset(warm[:], 0.0)
         for t in range(NT):
-            nc.vector.memset(windows[t][:, 0:T], 0.0)
+            nc.vector.memset(windows[t][:], 0.0)
 
         x_rows = xT.rearrange("(p j) t -> p j t", j=4)
 
         def load_scales(tile, src):
             for g in range(4):
                 nc.sync.dma_start(
-                    tile[32 * g : 32 * g + 4, 0:E, :].bitcast(I32),
+                    tile[32 * g : 32 * g + 4, :, :].bitcast(I32),
                     src[:, 0, 4 * g : 4 * g + 4, :].rearrange("e q i -> q e i").bitcast(I32),
                 )
 
-        def load_words(tile, src, e0, e1):
-            nc.sync.dma_start(tile[:, 0 : e1 - e0, :].bitcast(I32), src[e0:e1, 0].rearrange("e p n -> p e n").bitcast(I32))
+        def load_words(tile, src, e0):
+            nc.sync.dma_start(tile[:].bitcast(I32), src[e0 : e0 + 2, 0].rearrange("e p n -> p e n").bitcast(I32))
 
         nc.scalar.activation(out=warm[:], in_=warm[:], func=RELU)
 
@@ -86,14 +78,16 @@ def tile_moe_res_glu_relu_kernel(
             nc.sync.dma_start(raw[:], x_rows[:, :, a:b])
         nc.sync.dma_start(offsets[:], offs)
         load_scales(w1s, w1_scales)
-        load_words(w1w[0], w1_words, 0, 2)
-        load_words(w3w[0], w3_words, 0, 2)
+        load_words(w1w[0], w1_words, 0)
+        load_words(w3w[0], w3_words, 0)
         load_scales(w3s, w3_scales)
-        load_words(w1w[1], w1_words, 2, 4)
-        load_words(w3w[1], w3_words, 2, 4)
-        load_words(w2w, w2_words, 0, E)
+        load_words(w1w[1], w1_words, 2)
+        load_words(w3w[1], w3_words, 2)
+        nc.sync.dma_start(gates[0][:], gate[0:P, 0 : 2 * C])
+        load_words(w2w[0], w2_words, 0)
         load_scales(w2s, w2_scales)
-        nc.sync.dma_start(gate_t[:], gate[0:P, :])
+        load_words(w2w[1], w2_words, 2)
+        nc.sync.dma_start(gates[1][:], gate[0:P, 2 * C : 4 * C])
         nc.sync.dma_start(res[:], xr.rearrange("(t p) c -> p t c", p=P))
 
         def round_tokens(copy, grouped, raw, a, b):
@@ -112,198 +106,133 @@ def tile_moe_res_glu_relu_kernel(
                 scales=scales[:, a:b],
                 in_=grouped[:].rearrange("p w j -> p (w j)"),
             )
-            if a == 0:
-                hs_all = held.tile([P, E * C], U8, name="grouped0", align_bytes=64)
-                nc.vector.memset(hs_all[:].bitcast(I32), 0)
-                for i in range(3):
-                    nc.tensor.matmul_mx(
-                        out=banks[5 + i][:],
-                        lhsT=w2w[:, E, 0 : 2 * P].bitcast(FP4X4),
-                        lhsT_scale=w2s[:, E, 0:P],
-                        rhs=hc_all[:].bitcast(FP8X4),
-                        rhs_scale=hs_all[:],
-                        start=True,
-                        stop=True,
-                    )
 
         def slots_of(e0, e1):
             return offsets[:, e0 * LIST_COLS : e1 * LIST_COLS]
 
-        token_words = {}
-
-        token_scales = {}
-
-        def gather_words(e0, e1, buffer):
-            words = held.tile([P, (e1 - e0) * C], U32, name=buffer, align_bytes=64)
-            nc.vector.tensor_copy(words[:], codes[:].indirect(slots_of(e0, e1)))
-            for e in range(e0, e1):
-                token_words[e] = words[:, (e - e0) * C : (e - e0 + 1) * C]
-
-        def gather_scales(e0, e1, buffer):
-            planes = held.tile([P, (e1 - e0) * C], U8, name=buffer, align_bytes=64)
-            nc.vector.tensor_copy(planes[:], scales[:].indirect(slots_of(e0, e1)))
-            for e in range(e0, e1):
-                token_scales[e] = planes[:, (e - e0) * C : (e - e0 + 1) * C]
-
+        tokens = {}
         hidden = {}
         hidden_mx = {}
+        rectified = {}
 
-        def layer1(e, pa, pb):
-            multiply1(e, pa, pb)
-            gate_units(e, pa, pb)
+        def gather(e, buffer):
+            words = held.tile([P, C], U32, name=f"words{buffer}", align_bytes=64)
+            planes = held.tile([P, C], U8, name=f"planes{buffer}", align_bytes=64)
+            nc.vector.tensor_copy(words[:], codes[:].indirect(slots_of(e, e + 1)))
+            nc.vector.tensor_copy(planes[:], scales[:].indirect(slots_of(e, e + 1)))
+            tokens[e] = (words, planes)
 
-        def multiply1(e, pa, pb):
-            for acc, words, sc in ((pa, w1w, w1s), (pb, w3w, w3s)):
-                nc.tensor.matmul_mx(
-                    out=acc[:],
-                    lhsT=token_words[e].bitcast(FP8X4),
-                    lhsT_scale=token_scales[e],
-                    rhs=words[e // 2][:, e % 2, :].bitcast(FP4X4),
-                    rhs_scale=sc[:, e, :],
-                    start=True,
-                    stop=True,
-                )
+        def multiply1(e, acc, words, sc):
+            nc.tensor.matmul_mx(
+                out=acc[:],
+                lhsT=tokens[e][0][:].bitcast(FP8X4),
+                lhsT_scale=tokens[e][1][:],
+                rhs=words[e // 2][:, e % 2, :].bitcast(FP4X4),
+                rhs_scale=sc[:, e, :],
+                start=True,
+                stop=True,
+            )
 
-        def gate_units(e, pa, pb):
-            a_pairs, b_pairs = [acc[:].rearrange("s (p u d) -> s u p d", u=2, d=2) for acc in (pa, pb)]
-            h = held.tile([P, 2, P, 2], BF16, name="words1" if e == 2 else f"h{e}", align_bytes=64)
-            ra = work.tile([P, 2, P, 2], F32, name="ra", bufs=3)
-            nc.scalar.activation(out=ra[:], in_=a_pairs, func=RELU)
-            nc.vector.tensor_tensor(out=h[:], in0=b_pairs, in1=ra[:], op=MULT)
+        def pairs_of(acc):
+            return acc[:].rearrange("s (p u d) -> s u p d", u=2, d=2)
+
+        def rectify(e, bank):
+            multiply1(e, bank, w1w, w1s)
+            ra = held.tile([P, 2, P, 2], F32, name=f"ra{e}")
+            nc.scalar.activation(out=ra[:], in_=pairs_of(bank), func=RELU)
+            rectified[e] = ra
+
+        def gate_units(e, bank):
+            multiply1(e, bank, w3w, w3s)
+            if e == E - 1:
+                h = values[:, place[2, 1] : place[2, 1] + 2 * C].bitcast(BF16).rearrange("s (u p d) -> s u p d", u=2, d=2)
+            else:
+                h = held.tile([P, 2, P, 2], BF16, name=f"h{e}", align_bytes=64)[:]
+            nc.vector.tensor_tensor(out=h, in0=pairs_of(bank), in1=rectified[e][:], op=MULT)
             hidden[e] = h
 
-        def turn(e0, e1, bank):
-            n = e1 - e0
-            ph = bank[:, 0 : n * 2 * C].rearrange("p (e u c) -> p e u c", e=n, u=2)
-            for e in range(e0, e1):
-                for u in range(2):
-                    pairs = hidden[e][:, u, :, :].rearrange("s p d -> s (p d)").bitcast(F32)
-                    nc.tensor.transpose(ph[:, e - e0, u, :], pairs, ident[:])
-            hg = work.tile([P, n, C, 4], BF16, name="hg", align_bytes=64)
+        def turn(e, bank):
+            ph = bank[:, 0 : 2 * C].rearrange("p (u c) -> p u c", u=2)
+            for u in range(2):
+                pairs = hidden[e][:, u, :, :].rearrange("s p d -> s (p d)").bitcast(F32)
+                nc.tensor.transpose(ph[:, u, :], pairs, ident[:])
+            hg = held.tile([P, C, 4], BF16, name=f"hg{e}", align_bytes=64)
             nc.scalar.copy(
-                out=hg[:].rearrange("p e c j -> p (e c j)").bitcast(F32).rearrange("p (e c u) -> p e c u", e=n, u=2),
-                in_=ph.rearrange("p e u c -> p e c u"),
+                out=hg[:].rearrange("p c j -> p (c j)").bitcast(F32).rearrange("p (c u) -> p c u", u=2),
+                in_=ph.rearrange("p u c -> p c u"),
             )
-            hc = hc_all[:, e0 * C : e1 * C]
-            hs = hs_all[:, e0 * C : e1 * C]
-            nc.vector.quantize_mx(
-                out=hc.bitcast(FP8X4), scales=hs, in_=hg[:].rearrange("p e c j -> p (e c j)")
-            )
-            for e in range(e0, e1):
-                cols = slice((e - e0) * C, (e - e0 + 1) * C)
-                hidden_mx[e] = (hc[:, cols], hs[:, cols])
+            hc = held.tile([P, C], U32, name=f"hc{e}", align_bytes=64)
+            hs = held.tile([P, C], U8, name=f"hs{e}", align_bytes=64)
+            nc.vector.quantize_mx(out=hc[:].bitcast(FP8X4), scales=hs[:], in_=hg[:].rearrange("p c j -> p (c j)"))
+            hidden_mx[e] = (hc, hs)
 
-        y0 = held.tile([P, 3, C], F32, name="y0")
-        y1 = held.tile([P, 3, C], F32, name="y1")
-        y23 = held.tile([P, 2, C], F32, name="y23")
-        gate_cols = held.tile([P, E, 1], F32, name="gate_cols")
-        by_slot = {}
+        order = [(0, 0), (2, 0), (2, 1), (0, 1)] + [(1, e) for e in range(E)] + [(0, 2), (0, 3), (2, 2), (2, 3)] + [(3, e) for e in range(E)]
+        place = {block: b * C for b, block in enumerate(order)}
 
-        def layer2(experts, tiles, bank):
-            blocks = [(e, t) for t in tiles for e in experts]
-            py = bank[:, 0 : len(blocks) * C].rearrange("p (b c) -> p b c", c=C)
-            for b, (e, t) in enumerate(blocks):
+        def layer2(tiles, e0, e1, bank):
+            blocks = [(t, e) for t in tiles for e in range(e0, e1)]
+            for b, (t, e) in sorted(enumerate(blocks), key=lambda be: be[1][1]):
                 hc, hs = hidden_mx[e]
                 nc.tensor.matmul_mx(
-                    out=py[:, b, :],
-                    lhsT=w2w[:, e, t * 2 * P : (t + 1) * 2 * P].bitcast(FP4X4),
+                    out=bank[:, b * C : (b + 1) * C],
+                    lhsT=w2w[e // 2][:, e % 2, t * 2 * P : (t + 1) * 2 * P].bitcast(FP4X4),
                     lhsT_scale=w2s[:, e, t * P : (t + 1) * P],
-                    rhs=hc.bitcast(FP8X4),
-                    rhs_scale=hs,
+                    rhs=hc[:].bitcast(FP8X4),
+                    rhs_scale=hs[:],
                     start=True,
                     stop=True,
                 )
-            return py
-
-        def turn_gate(bank):
-            turned_gate = bank[:].rearrange("p (e c) -> p e c", e=E)
-            for e in range(E):
-                nc.tensor.transpose(turned_gate[:, e, :], gate_t[:, e * C : (e + 1) * C], ident[:])
-            nc.scalar.copy(out=gate_cols[:], in_=turned_gate[:, :, 0:1])
-
-        def layer2_by_slot(e, t0, bank_cols):
-            hc, hs = hidden_mx[e]
-            for t in range(t0, NT):
-                nc.tensor.matmul_mx(
-                    out=bank_cols[:, (t - t0) * P : (t - t0 + 1) * P],
-                    lhsT=hc.bitcast(FP8X4),
-                    lhsT_scale=hs,
-                    rhs=w2w[:, e, t * 2 * P : (t + 1) * 2 * P].bitcast(FP4X4),
-                    rhs_scale=w2s[:, e, t * P : (t + 1) * P],
-                    start=True,
-                    stop=True,
-                )
-            gated = held.tile([P, (NT - t0) * P], F32, name=f"gated{e}")
-            nc.scalar.activation(out=gated[:], in_=bank_cols, func=COPY, scale=gate_cols[:, e, :])
-            for t in range(t0, NT):
-                by_slot[e, t] = gated[:, (t - t0) * P : (t - t0 + 1) * P]
-
-        def turn_gated(t, e0, bank):
-            cols = bank[:, 0 : (E - e0) * C]
-            for e in range(e0, E):
-                nc.tensor.transpose(cols[:, (e - e0) * C : (e - e0 + 1) * C], by_slot[e, t], ident[:])
-            values = held.tile([P, (E - e0) * C], F32, name=f"values{t}")
-            nc.scalar.copy(out=values[:], in_=cols)
-            return values
-
-        def scatter_gated(t, e0, values):
-            nc.vector.tensor_copy(windows[t][:].indirect(slots_of(e0, E)), values[:])
-
-        def scatter(t, e0, e1, values):
+            width = (e1 - e0) * C
+            cols = len(blocks) * C
+            first, last = [place[t, e0] // width for t in tiles]
             nc.vector.tensor_tensor(
-                windows[t][:].indirect(slots_of(e0, e1)),
-                values,
-                gate_t[:, e0 * C : e1 * C],
-                MULT,
+                out=values[:].rearrange("p (t c) -> p t c", c=width)[:, first : last + 1 : last - first, :],
+                in0=bank[:, 0:cols].rearrange("p (t c) -> p t c", c=width),
+                in1=gates[e0 // 2][:, e0 % 2 * C : e0 % 2 * C + width].unsqueeze(1).to_broadcast([P, len(tiles), width]),
+                op=MULT,
             )
 
-        def add_by_gpsimd(t):
-            o = held.tile([P, T], F32, name=f"gated{t}")
-            nc.gpsimd.tensor_tensor(out=o[:], in0=windows[t][:, 0:T], in1=res[:, t, :], op=ADD)
-            nc.scalar.dma_start(out[t * P : (t + 1) * P, :], o[:])
+        def source(t, e0, e1):
+            return values[:, place[t, e0] : place[t, e0] + (e1 - e0) * C]
 
-        def add_by_vector(t):
+        def scatter_by_vector(t, e0, e1):
+            nc.vector.tensor_copy(windows[t][:].indirect(slots_of(e0, e1)), source(t, e0, e1))
+
+        def scatter_by_scalar(t, e0, e1):
+            nc.scalar.activation(windows[t][:].indirect(slots_of(e0, e1)), source(t, e0, e1), COPY)
+
+        def add_and_store(add, t, parts):
             o = held.tile([P, T], F32, name=f"sum{t}")
-            for a, b in LAST_PARTS:
-                cols = slice(a, b)
-                nc.vector.tensor_tensor(out=o[:, cols], in0=windows[t][:, cols], in1=res[:, t, cols], op=ADD)
-                nc.sync.dma_start(out[t * P : (t + 1) * P, cols], o[:, cols])
+            for a, b in parts:
+                add(out=o[:, a:b], in0=windows[t][:, a:b], in1=res[:, t, a:b], op=ADD)
+                nc.sync.dma_start(out[t * P : (t + 1) * P, a:b], o[:, a:b])
 
-        gather_words(0, 1, "words0")
-        gather_scales(0, 1, "planes0")
-        gather_words(1, 2, "words1")
-        gather_scales(1, 2, "planes1")
-        gather_words(2, 3, "words2")
-        gather_scales(2, E, "planes2")
-        layer1(0, banks[0], banks[1])
-        multiply1(1, banks[2], banks[3])
-        gather_words(LAST_E, E, "words1")
-        gate_units(1, banks[2], banks[3])
-        turn(0, 1, banks[7])
-        multiply1(2, banks[4], banks[5])
-        multiply1(3, banks[0], banks[6])
-        gate_units(2, banks[4], banks[5])
-        nc.scalar.copy(out=y0[:, 0:1, :], in_=layer2([0], [0], banks[4]))
-        nc.scalar.copy(out=y0[:, 1:3, :], in_=layer2([0], [1, 2], banks[1]))
-        turn(1, 2, banks[2])
-        gate_units(3, banks[0], banks[6])
-        turn(2, 4, banks[4])
-        nc.scalar.copy(out=y1[:], in_=layer2([1], range(3), banks[4]))
-        turn_gate(banks[1])
-        nc.scalar.copy(out=y23[:], in_=layer2([2, 3], [0], banks[5]))
-        layer2_by_slot(2, 1, banks[7][:, 0 : 3 * P])
-        layer2_by_slot(3, 1, banks[0][:, 0 : 3 * P])
-        values1 = turn_gated(1, 2, banks[2])
-        values2 = turn_gated(2, 2, banks[3])
-        layer2_by_slot(1, 3, banks[4][:, 0:P])
-        layer2_by_slot(0, 3, banks[5][:, 0:P])
-        values3 = turn_gated(3, 0, banks[6])
-        for t in range(LAST):
-            scatter(t, 0, 1, y0[:, t, :])
-        for t in range(LAST):
-            scatter(t, 1, 2, y1[:, t, :])
-        scatter(0, 2, E, y23[:].rearrange("p e c -> p (e c)"))
-        for t, (e0, values) in enumerate(((2, values1), (2, values2), (0, values3))):
-            add_by_gpsimd(t)
-            scatter_gated(t + 1, e0, values)
-        add_by_vector(LAST)
+        for e in range(E):
+            gather(e, e)
+        for e0 in (0, 2):
+            for e in (e0, e0 + 1):
+                rectify(e, banks[2 * e0 + e % 2])
+            for e in (e0, e0 + 1):
+                gate_units(e, banks[2 * e0 + 2 + e % 2])
+        turn(0, banks[0])
+        turn(1, banks[1])
+        turn(2, banks[4])
+        layer2([0, 2], 0, 1, banks[2])
+        turn(3, banks[5])
+        scatter_by_scalar(0, 0, 1)
+        layer2([2, 0], 1, 2, banks[3])
+        layer2([1, 3], 0, 2, banks[7])
+        scatter_by_scalar(0, 1, 2)
+        scatter_by_scalar(2, 0, 2)
+        layer2([1, 0], 2, 4, banks[6])
+        layer2([2, 3], 2, 4, banks[0])
+        scatter_by_scalar(0, 2, 4)
+        scatter_by_vector(1, 0, 3)
+        scatter_by_vector(1, 3, 4)
+        scatter_by_scalar(3, 0, 3)
+        scatter_by_scalar(3, 3, 4)
+        scatter_by_vector(2, 2, 4)
+        add_and_store(nc.gpsimd.tensor_tensor, 0, ((0, T),))
+        add_and_store(nc.gpsimd.tensor_tensor, 1, ((0, T),))
+        add_and_store(nc.vector.tensor_tensor, 2, ((0, T),))
+        add_and_store(nc.vector.tensor_tensor, 3, LAST_PARTS)

@@ -6,10 +6,12 @@ from concourse.masks import make_identity
 K, T, E, C, H, N = 512, 640, 4, 128, 512, 512
 P = 128
 NT = N // P
-LIST_COLS = C // 16
+SHARED_SPLIT = 160
+WIDE = 704
 CHUNKS = ((0, 256), (256, 512), (512, T))
 VECTOR_EIGHTHS = 5
-LAST_PARTS = ((0, 128), (128, 384), (384, T))
+LAST_PARTS = ((0, 256), (256, 512), (512, T))
+HALVES = ((0, T // 2), (T // 2, T))
 
 FLOPS = 3 * 2 * E * C * K * H
 BYTES = 2 * K * T * 4 + N * T * 4 + 3 * E * (P * 1024 + 16 * 512) + E * C * 4 + P * 64
@@ -38,27 +40,24 @@ def tile_moe_res_glu_relu_kernel(
         banks = [psum.tile([P, 512], F32, name=f"bank{i}") for i in range(8)]
 
         offsets = held.tile([P, E * C // 16], U16, name="offsets")
-        gates = [held.tile([P, 2 * C], F32, name=f"gate{g}") for g in range(2)]
+        gate_t = held.tile([P, E * C], F32, name="gate_t")
         ident = held.tile([P, P], F32, name="ident")
         warm = held.tile([P, 1], F32, name="warm")
         codes = held.tile([P, T], U32, name="codes", align_bytes=64)
         scales = held.tile([P, T], U8, name="scales", align_bytes=64)
-        w1w = [held.tile([P, 2, 2 * H], U8, name=f"w1w{g}", align_bytes=64) for g in range(2)]
-        w3w = [held.tile([P, 2, 2 * H], U8, name=f"w3w{g}", align_bytes=64) for g in range(2)]
-        w2w = [held.tile([P, 2, 2 * N], U8, name=f"w2w{g}", align_bytes=64) for g in range(2)]
+        w1w, w3w, w2w = {}, {}, {}
         w1s = held.tile([P, E, H], U8, name="w1s", align_bytes=64)
         w3s = held.tile([P, E, H], U8, name="w3s", align_bytes=64)
         w2s = held.tile([P, E, N], U8, name="w2s", align_bytes=64)
         res = held.tile([P, NT, T], F32, name="res")
         raws = [held.tile([P, 4, b - a], F32, name=f"raw{a}", align_bytes=64) for a, b in CHUNKS]
-        windows = [held.tile([P, T], F32, name=f"window{t}") for t in range(NT)]
-        values = held.tile([P, NT * E * C], F32, name="values", align_bytes=64)
+        windows = [held.tile([P, WIDE if t == 1 else T], F32, name=f"window{t}") for t in range(NT)]
 
         nc.gpsimd.memset(scales[:].bitcast(I32), 0)
         make_identity(nc, ident[:])
         nc.vector.memset(warm[:], 0.0)
         for t in range(NT):
-            nc.vector.memset(windows[t][:], 0.0)
+            nc.vector.memset(windows[t][:, 0:T], 0.0)
 
         x_rows = xT.rearrange("(p j) t -> p j t", j=4)
 
@@ -69,8 +68,11 @@ def tile_moe_res_glu_relu_kernel(
                     src[:, 0, 4 * g : 4 * g + 4, :].rearrange("e q i -> q e i").bitcast(I32),
                 )
 
-        def load_words(tile, src, e0):
-            nc.sync.dma_start(tile[:].bitcast(I32), src[e0 : e0 + 2, 0].rearrange("e p n -> p e n").bitcast(I32))
+        def load_words(words, name, src, e0, e1):
+            tile = held.tile([P, e1 - e0, 2 * H], U8, name=f"{name}_{e0}", align_bytes=64)
+            nc.sync.dma_start(tile[:].bitcast(I32), src[e0:e1, 0].rearrange("e p n -> p e n").bitcast(I32))
+            for e in range(e0, e1):
+                words[e] = tile[:, e - e0, :]
 
         nc.scalar.activation(out=warm[:], in_=warm[:], func=RELU)
 
@@ -78,16 +80,15 @@ def tile_moe_res_glu_relu_kernel(
             nc.sync.dma_start(raw[:], x_rows[:, :, a:b])
         nc.sync.dma_start(offsets[:], offs)
         load_scales(w1s, w1_scales)
-        load_words(w1w[0], w1_words, 0)
-        load_words(w3w[0], w3_words, 0)
+        load_words(w1w, "w1", w1_words, 0, 2)
+        load_words(w3w, "w3", w3_words, 0, 2)
         load_scales(w3s, w3_scales)
-        load_words(w1w[1], w1_words, 2)
-        load_words(w3w[1], w3_words, 2)
-        nc.sync.dma_start(gates[0][:], gate[0:P, 0 : 2 * C])
-        load_words(w2w[0], w2_words, 0)
+        load_words(w1w, "w1", w1_words, 2, 4)
+        load_words(w3w, "w3", w3_words, 2, 4)
+        nc.sync.dma_start(gate_t[:], gate[0:P, :])
+        load_words(w2w, "w2", w2_words, 0, 2)
         load_scales(w2s, w2_scales)
-        load_words(w2w[1], w2_words, 2)
-        nc.sync.dma_start(gates[1][:], gate[0:P, 2 * C : 4 * C])
+        load_words(w2w, "w2", w2_words, 2, 4)
         nc.sync.dma_start(res[:], xr.rearrange("(t p) c -> p t c", p=P))
 
         def round_tokens(copy, grouped, raw, a, b):
@@ -107,27 +108,29 @@ def tile_moe_res_glu_relu_kernel(
                 in_=grouped[:].rearrange("p w j -> p (w j)"),
             )
 
-        def slots_of(e0, e1):
-            return offsets[:, e0 * LIST_COLS : e1 * LIST_COLS]
+        def slots(a, b):
+            return offsets[:, a // 16 : b // 16]
 
         tokens = {}
         hidden = {}
         hidden_mx = {}
         rectified = {}
 
-        def gather(e, buffer):
-            words = held.tile([P, C], U32, name=f"words{buffer}", align_bytes=64)
-            planes = held.tile([P, C], U8, name=f"planes{buffer}", align_bytes=64)
-            nc.vector.tensor_copy(words[:], codes[:].indirect(slots_of(e, e + 1)))
-            nc.vector.tensor_copy(planes[:], scales[:].indirect(slots_of(e, e + 1)))
-            tokens[e] = (words, planes)
+        def gather(e0, e1):
+            words = held.tile([P, (e1 - e0) * C], U32, name=f"words{e0}", align_bytes=64)
+            planes = held.tile([P, (e1 - e0) * C], U8, name=f"planes{e0}", align_bytes=64)
+            nc.vector.tensor_copy(words[:], codes[:].indirect(slots(e0 * C, e1 * C)))
+            nc.vector.tensor_copy(planes[:], scales[:].indirect(slots(e0 * C, e1 * C)))
+            for e in range(e0, e1):
+                cols = slice((e - e0) * C, (e - e0 + 1) * C)
+                tokens[e] = (words[:, cols], planes[:, cols])
 
         def multiply1(e, acc, words, sc):
             nc.tensor.matmul_mx(
                 out=acc[:],
-                lhsT=tokens[e][0][:].bitcast(FP8X4),
-                lhsT_scale=tokens[e][1][:],
-                rhs=words[e // 2][:, e % 2, :].bitcast(FP4X4),
+                lhsT=tokens[e][0].bitcast(FP8X4),
+                lhsT_scale=tokens[e][1],
+                rhs=words[e].bitcast(FP4X4),
                 rhs_scale=sc[:, e, :],
                 start=True,
                 stop=True,
@@ -144,10 +147,7 @@ def tile_moe_res_glu_relu_kernel(
 
         def gate_units(e, bank):
             multiply1(e, bank, w3w, w3s)
-            if e == E - 1:
-                h = values[:, place[2, 1] : place[2, 1] + 2 * C].bitcast(BF16).rearrange("s (u p d) -> s u p d", u=2, d=2)
-            else:
-                h = held.tile([P, 2, P, 2], BF16, name=f"h{e}", align_bytes=64)[:]
+            h = held.tile([P, 2, P, 2], BF16, name=f"h{e}", align_bytes=64)[:]
             nc.vector.tensor_tensor(out=h, in0=pairs_of(bank), in1=rectified[e][:], op=MULT)
             hidden[e] = h
 
@@ -166,73 +166,63 @@ def tile_moe_res_glu_relu_kernel(
             nc.vector.quantize_mx(out=hc[:].bitcast(FP8X4), scales=hs[:], in_=hg[:].rearrange("p c j -> p (c j)"))
             hidden_mx[e] = (hc, hs)
 
-        order = [(0, 0), (2, 0), (2, 1), (0, 1)] + [(1, e) for e in range(E)] + [(0, 2), (0, 3), (2, 2), (2, 3)] + [(3, e) for e in range(E)]
-        place = {block: b * C for b, block in enumerate(order)}
+        values = [held.tile([P, E * C], F32, name=f"values{t}") for t in range(NT)]
 
-        def layer2(tiles, e0, e1, bank):
-            blocks = [(t, e) for t in tiles for e in range(e0, e1)]
-            for b, (t, e) in sorted(enumerate(blocks), key=lambda be: be[1][1]):
-                hc, hs = hidden_mx[e]
-                nc.tensor.matmul_mx(
-                    out=bank[:, b * C : (b + 1) * C],
-                    lhsT=w2w[e // 2][:, e % 2, t * 2 * P : (t + 1) * 2 * P].bitcast(FP4X4),
-                    lhsT_scale=w2s[:, e, t * P : (t + 1) * P],
-                    rhs=hc[:].bitcast(FP8X4),
-                    rhs_scale=hs[:],
-                    start=True,
-                    stop=True,
-                )
-            width = (e1 - e0) * C
-            cols = len(blocks) * C
-            first, last = [place[t, e0] // width for t in tiles]
-            nc.vector.tensor_tensor(
-                out=values[:].rearrange("p (t c) -> p t c", c=width)[:, first : last + 1 : last - first, :],
-                in0=bank[:, 0:cols].rearrange("p (t c) -> p t c", c=width),
-                in1=gates[e0 // 2][:, e0 % 2 * C : e0 % 2 * C + width].unsqueeze(1).to_broadcast([P, len(tiles), width]),
-                op=MULT,
+        def multiply2(t, e, acc):
+            hc, hs = hidden_mx[e]
+            nc.tensor.matmul_mx(
+                out=acc,
+                lhsT=w2w[e][:, t * 2 * P : (t + 1) * 2 * P].bitcast(FP4X4),
+                lhsT_scale=w2s[:, e, t * P : (t + 1) * P],
+                rhs=hc[:].bitcast(FP8X4),
+                rhs_scale=hs[:],
+                start=True,
+                stop=True,
             )
 
-        def source(t, e0, e1):
-            return values[:, place[t, e0] : place[t, e0] + (e1 - e0) * C]
+        def layer2(t, e0, e1, bank):
+            for e in range(e0, e1):
+                multiply2(t, e, bank[:, (e - e0) * C : (e - e0 + 1) * C])
+            cols = slice(e0 * C, e1 * C)
+            nc.vector.tensor_tensor(out=values[t][:, cols], in0=bank[:, 0 : (e1 - e0) * C], in1=gate_t[:, cols], op=MULT)
 
-        def scatter_by_vector(t, e0, e1):
-            nc.vector.tensor_copy(windows[t][:].indirect(slots_of(e0, e1)), source(t, e0, e1))
+        def scatter_by_vector(t, a, b):
+            nc.vector.tensor_copy(windows[t][:].indirect(slots(a, b)), values[t][:, a:b])
 
-        def scatter_by_scalar(t, e0, e1):
-            nc.scalar.activation(windows[t][:].indirect(slots_of(e0, e1)), source(t, e0, e1), COPY)
+        def scatter_by_scalar(t, a, b):
+            nc.scalar.activation(windows[t][:].indirect(slots(a, b)), values[t][:, a:b], COPY)
 
-        def add_and_store(add, t, parts):
-            o = held.tile([P, T], F32, name=f"sum{t}")
+        def add_and_store(add, t, parts, o):
             for a, b in parts:
                 add(out=o[:, a:b], in0=windows[t][:, a:b], in1=res[:, t, a:b], op=ADD)
                 nc.sync.dma_start(out[t * P : (t + 1) * P, a:b], o[:, a:b])
 
-        for e in range(E):
-            gather(e, e)
+        gather(0, 1)
+        gather(1, 2)
+        gather(2, 4)
         for e0 in (0, 2):
             for e in (e0, e0 + 1):
                 rectify(e, banks[2 * e0 + e % 2])
             for e in (e0, e0 + 1):
                 gate_units(e, banks[2 * e0 + 2 + e % 2])
-        turn(0, banks[0])
-        turn(1, banks[1])
-        turn(2, banks[4])
-        layer2([0, 2], 0, 1, banks[2])
+        turn(0, banks[4])
+        turn(1, banks[0])
+        turn(2, banks[1])
         turn(3, banks[5])
-        scatter_by_scalar(0, 0, 1)
-        layer2([2, 0], 1, 2, banks[3])
-        layer2([1, 3], 0, 2, banks[7])
-        scatter_by_scalar(0, 1, 2)
-        scatter_by_scalar(2, 0, 2)
-        layer2([1, 0], 2, 4, banks[6])
-        layer2([2, 3], 2, 4, banks[0])
-        scatter_by_scalar(0, 2, 4)
-        scatter_by_vector(1, 0, 3)
-        scatter_by_vector(1, 3, 4)
-        scatter_by_scalar(3, 0, 3)
-        scatter_by_scalar(3, 3, 4)
-        scatter_by_vector(2, 2, 4)
-        add_and_store(nc.gpsimd.tensor_tensor, 0, ((0, T),))
-        add_and_store(nc.gpsimd.tensor_tensor, 1, ((0, T),))
-        add_and_store(nc.vector.tensor_tensor, 2, ((0, T),))
-        add_and_store(nc.vector.tensor_tensor, 3, LAST_PARTS)
+        layer2(0, 0, 2, banks[2])
+        layer2(1, 0, 2, banks[3])
+        layer2(0, 2, 4, banks[6])
+        layer2(1, 2, 4, banks[7])
+        layer2(2, 0, 4, banks[4])
+        layer2(3, 0, 4, banks[0])
+        scatter_by_scalar(0, 0, 2 * C)
+        scatter_by_scalar(0, 2 * C, 4 * C)
+        scatter_by_scalar(2, 0, SHARED_SPLIT)
+        scatter_by_scalar(3, 0, 3 * C)
+        scatter_by_scalar(3, 3 * C, 4 * C)
+        scatter_by_vector(1, 0, 4 * C)
+        scatter_by_vector(2, SHARED_SPLIT, 4 * C)
+        add_and_store(nc.gpsimd.tensor_tensor, 0, ((0, T),), held.tile([P, T], F32, name="sum0"))
+        add_and_store(nc.gpsimd.tensor_tensor, 1, ((0, T),), held.tile([P, T], F32, name="sum1"))
+        add_and_store(nc.vector.tensor_tensor, 2, HALVES, res[:, 1, :])
+        add_and_store(nc.vector.tensor_tensor, 3, LAST_PARTS, held.tile([P, T], F32, name="window1"))

@@ -168,10 +168,10 @@ def tile_moe_res_glu_relu_kernel(
 
         values = [held.tile([P, E * C], F32, name=f"values{t}") for t in range(NT)]
 
-        def multiply2(t, e, acc):
+        def multiply2(t, e, bank):
             hc, hs = hidden_mx[e]
             nc.tensor.matmul_mx(
-                out=acc,
+                out=bank[:, e * C : (e + 1) * C],
                 lhsT=w2w[e][:, t * 2 * P : (t + 1) * 2 * P].bitcast(FP4X4),
                 lhsT_scale=w2s[:, e, t * P : (t + 1) * P],
                 rhs=hc[:].bitcast(FP8X4),
@@ -180,11 +180,9 @@ def tile_moe_res_glu_relu_kernel(
                 stop=True,
             )
 
-        def layer2(t, e0, e1, bank):
-            for e in range(e0, e1):
-                multiply2(t, e, bank[:, (e - e0) * C : (e - e0 + 1) * C])
+        def apply_gate(t, e0, e1, bank):
             cols = slice(e0 * C, e1 * C)
-            nc.vector.tensor_tensor(out=values[t][:, cols], in0=bank[:, 0 : (e1 - e0) * C], in1=gate_t[:, cols], op=MULT)
+            nc.vector.tensor_tensor(out=values[t][:, cols], in0=bank[:, cols], in1=gate_t[:, cols], op=MULT)
 
         def scatter_by_vector(t, a, b):
             nc.vector.tensor_copy(windows[t][:].indirect(slots(a, b)), values[t][:, a:b])
@@ -209,12 +207,25 @@ def tile_moe_res_glu_relu_kernel(
         turn(1, banks[0])
         turn(2, banks[1])
         turn(3, banks[5])
-        layer2(0, 0, 2, banks[2])
-        layer2(1, 0, 2, banks[3])
-        layer2(0, 2, 4, banks[6])
-        layer2(1, 2, 4, banks[7])
-        layer2(2, 0, 4, banks[4])
-        layer2(3, 0, 4, banks[0])
+        early = {0: banks[2], 1: banks[3]}
+        late = {0: banks[6], 1: banks[7]}
+        whole = {2: banks[4], 3: banks[0]}
+        for t in (0, 1):
+            for e in (0, 1):
+                multiply2(t, e, early[t])
+            apply_gate(t, 0, 2, early[t])
+        for t in (0, 1):
+            multiply2(t, 2, late[t])
+        for e in (0, 1, 2):
+            multiply2(2, e, whole[2])
+        for t in (0, 1):
+            multiply2(t, 3, late[t])
+            apply_gate(t, 2, 4, late[t])
+        multiply2(2, 3, whole[2])
+        apply_gate(2, 0, 4, whole[2])
+        for e in range(E):
+            multiply2(3, e, whole[3])
+        apply_gate(3, 0, 4, whole[3])
         scatter_by_scalar(0, 0, 2 * C)
         scatter_by_scalar(0, 2 * C, 4 * C)
         scatter_by_scalar(2, 0, SHARED_SPLIT)

@@ -6,7 +6,7 @@ from concourse.masks import make_identity
 K, T, E, C, H, N = 512, 640, 4, 128, 512, 512
 P = 128
 NT = N // P
-SHARED_SPLIT = 160
+SHARED_SPLIT = 128
 WIDE = 704
 CHUNKS = ((0, 256), (256, 512), (512, T))
 VECTOR_EIGHTHS = 5
@@ -148,7 +148,10 @@ def tile_moe_res_glu_relu_kernel(
         def gate_units(e, bank):
             multiply1(e, bank, w3w, w3s)
             h = held.tile([P, 2, P, 2], BF16, name=f"h{e}", align_bytes=64)[:]
-            nc.vector.tensor_tensor(out=h, in0=pairs_of(bank), in1=rectified[e][:], op=MULT)
+            step = 1 if e == E - 1 else 2
+            for u in range(0, 2, step):
+                us = slice(u, u + step)
+                nc.vector.tensor_tensor(out=h[:, us], in0=pairs_of(bank)[:, us], in1=rectified[e][:, us], op=MULT)
             hidden[e] = h
 
         def turn(e, bank):
@@ -207,25 +210,21 @@ def tile_moe_res_glu_relu_kernel(
         turn(1, banks[0])
         turn(2, banks[1])
         turn(3, banks[5])
-        early = {0: banks[2], 1: banks[3]}
-        late = {0: banks[6], 1: banks[7]}
-        whole = {2: banks[4], 3: banks[0]}
-        for t in (0, 1):
+        early = {0: banks[2], 1: banks[3], 2: banks[4], 3: banks[0]}
+        late = {0: banks[6], 1: banks[7], 2: banks[1], 3: banks[0]}
+        for t in range(NT):
             for e in (0, 1):
                 multiply2(t, e, early[t])
-            apply_gate(t, 0, 2, early[t])
-        for t in (0, 1):
-            multiply2(t, 2, late[t])
-        for e in (0, 1, 2):
-            multiply2(2, e, whole[2])
-        for t in (0, 1):
-            multiply2(t, 3, late[t])
-            apply_gate(t, 2, 4, late[t])
-        multiply2(2, 3, whole[2])
-        apply_gate(2, 0, 4, whole[2])
-        for e in range(E):
-            multiply2(3, e, whole[3])
-        apply_gate(3, 0, 4, whole[3])
+            if t in (1, 2):
+                plain = held.tile([P, 2 * C], F32, name=f"plain{t}")
+                nc.scalar.copy(out=plain[:], in_=early[t][:, 0 : 2 * C])
+                nc.gpsimd.tensor_tensor(out=values[t][:, 0 : 2 * C], in0=plain[:], in1=gate_t[:, 0 : 2 * C], op=MULT)
+            elif t == 0:
+                apply_gate(t, 0, 2, early[t])
+        for t in range(NT):
+            for e in (2, 3):
+                multiply2(t, e, late[t])
+            apply_gate(t, 0 if t == 3 else 2, 4, late[t])
         scatter_by_scalar(0, 0, 2 * C)
         scatter_by_scalar(0, 2 * C, 4 * C)
         scatter_by_scalar(2, 0, SHARED_SPLIT)

@@ -6,7 +6,7 @@ from concourse.masks import make_identity
 K, T, E, C, H, N = 512, 640, 4, 128, 512, 512
 P = 128
 NT = N // P
-SHARED_SPLIT = 128
+SHARED_SPLIT = 96
 WIDE = 704
 CHUNKS = ((0, 256), (256, 512), (512, T))
 VECTOR_EIGHTHS = 5
@@ -211,7 +211,7 @@ def tile_moe_res_glu_relu_kernel(
         turn(2, banks[1])
         turn(3, banks[5])
         early = {0: banks[2], 1: banks[3], 2: banks[4], 3: banks[0]}
-        late = {0: banks[6], 1: banks[7], 2: banks[1], 3: banks[0]}
+        late = {0: banks[6], 1: banks[7], 2: banks[1], 3: banks[5]}
         for t in range(NT):
             for e in (0, 1):
                 multiply2(t, e, early[t])
@@ -219,12 +219,12 @@ def tile_moe_res_glu_relu_kernel(
                 plain = held.tile([P, 2 * C], F32, name=f"plain{t}")
                 nc.scalar.copy(out=plain[:], in_=early[t][:, 0 : 2 * C])
                 nc.gpsimd.tensor_tensor(out=values[t][:, 0 : 2 * C], in0=plain[:], in1=gate_t[:, 0 : 2 * C], op=MULT)
-            elif t == 0:
+            else:
                 apply_gate(t, 0, 2, early[t])
         for t in range(NT):
             for e in (2, 3):
                 multiply2(t, e, late[t])
-            apply_gate(t, 0 if t == 3 else 2, 4, late[t])
+            apply_gate(t, 2, 4, late[t])
         scatter_by_scalar(0, 0, 2 * C)
         scatter_by_scalar(0, 2 * C, 4 * C)
         scatter_by_scalar(2, 0, SHARED_SPLIT)

@@ -139,18 +139,20 @@ def tile_moe_res_glu_relu_kernel(
         def pairs_of(acc):
             return acc[:].rearrange("s (p u d) -> s u p d", u=2, d=2)
 
+        def halves(e):
+            return (slice(0, 1), slice(1, 2)) if e >= 2 else (slice(0, 2),)
+
         def rectify(e, bank):
             multiply1(e, bank, w1w, w1s)
             ra = held.tile([P, 2, P, 2], F32, name=f"ra{e}")
-            nc.scalar.activation(out=ra[:], in_=pairs_of(bank), func=RELU)
+            for us in halves(e):
+                nc.scalar.activation(out=ra[:, us], in_=pairs_of(bank)[:, us], func=RELU)
             rectified[e] = ra
 
         def gate_units(e, bank):
             multiply1(e, bank, w3w, w3s)
             h = held.tile([P, 2, P, 2], BF16, name=f"h{e}", align_bytes=64)[:]
-            step = 1 if e == E - 1 else 2
-            for u in range(0, 2, step):
-                us = slice(u, u + step)
+            for us in halves(e):
                 nc.vector.tensor_tensor(out=h[:, us], in0=pairs_of(bank)[:, us], in1=rectified[e][:, us], op=MULT)
             hidden[e] = h
 

@@ -8,8 +8,6 @@ P = 128
 NT = N // P
 SHARED_SPLIT = 96
 WIDE = 704
-CHUNKS = ((0, 256), (256, 512), (512, T))
-VECTOR_EIGHTHS = 5
 LAST_PARTS = ((0, 256), (256, 512), (512, T))
 HALVES = ((0, T // 2), (T // 2, T))
 
@@ -43,17 +41,14 @@ def tile_moe_res_glu_relu_kernel(
         gate_t = held.tile([P, E * C], F32, name="gate_t")
         ident = held.tile([P, P], F32, name="ident")
         warm = held.tile([P, 1], F32, name="warm")
-        codes = held.tile([P, T], U32, name="codes", align_bytes=64)
-        scales = held.tile([P, T], U8, name="scales", align_bytes=64)
         w1w, w3w, w2w = {}, {}, {}
         w1s = held.tile([P, E, H], U8, name="w1s", align_bytes=64)
         w3s = held.tile([P, E, H], U8, name="w3s", align_bytes=64)
         w2s = held.tile([P, E, N], U8, name="w2s", align_bytes=64)
         res = held.tile([P, NT, T], F32, name="res")
-        raws = [held.tile([P, 4, b - a], F32, name=f"raw{a}", align_bytes=64) for a, b in CHUNKS]
+        planes = [held.tile([P, T], F32, name=f"plane{j}", align_bytes=64) for j in range(4)]
         windows = [held.tile([P, WIDE if t == 1 else T], F32, name=f"window{t}") for t in range(NT)]
 
-        nc.gpsimd.memset(scales[:].bitcast(I32), 0)
         make_identity(nc, ident[:])
         nc.vector.memset(warm[:], 0.0)
         for t in range(NT):
@@ -76,9 +71,9 @@ def tile_moe_res_glu_relu_kernel(
 
         nc.scalar.activation(out=warm[:], in_=warm[:], func=RELU)
 
-        for raw, (a, b) in zip(raws, CHUNKS):
-            nc.sync.dma_start(raw[:], x_rows[:, :, a:b])
         nc.sync.dma_start(offsets[:], offs)
+        for j in range(4):
+            nc.sync.dma_start(planes[j][:], x_rows[:, j, :])
         load_scales(w1s, w1_scales)
         load_words(w1w, "w1", w1_words, 0, 2)
         load_words(w3w, "w3", w3_words, 0, 2)
@@ -91,23 +86,6 @@ def tile_moe_res_glu_relu_kernel(
         load_words(w2w, "w2", w2_words, 2, 4)
         nc.sync.dma_start(res[:], xr.rearrange("(t p) c -> p t c", p=P))
 
-        def round_tokens(copy, grouped, raw, a, b):
-            copy(
-                out=grouped[:, a:b, :].rearrange("p (c i) j -> p c j i", i=4),
-                in_=raw[:, :, a:b].rearrange("p j (c i) -> p c j i", i=4),
-            )
-
-        for raw, (a, b) in zip(raws, CHUNKS):
-            grouped = held.tile([P, b - a, 4], BF16, name=f"grouped{a}", align_bytes=64)
-            share = (b - a) * VECTOR_EIGHTHS // 8
-            round_tokens(nc.vector.tensor_copy, grouped, raw, 0, share)
-            round_tokens(nc.scalar.copy, grouped, raw, share, b - a)
-            nc.vector.quantize_mx(
-                out=codes[:, a:b].bitcast(FP8X4),
-                scales=scales[:, a:b],
-                in_=grouped[:].rearrange("p w j -> p (w j)"),
-            )
-
         def slots(a, b):
             return offsets[:, a // 16 : b // 16]
 
@@ -116,14 +94,22 @@ def tile_moe_res_glu_relu_kernel(
         hidden_mx = {}
         rectified = {}
 
-        def gather(e0, e1):
-            words = held.tile([P, (e1 - e0) * C], U32, name=f"words{e0}", align_bytes=64)
-            planes = held.tile([P, (e1 - e0) * C], U8, name=f"planes{e0}", align_bytes=64)
-            nc.vector.tensor_copy(words[:], codes[:].indirect(slots(e0 * C, e1 * C)))
-            nc.vector.tensor_copy(planes[:], scales[:].indirect(slots(e0 * C, e1 * C)))
-            for e in range(e0, e1):
-                cols = slice((e - e0) * C, (e - e0 + 1) * C)
-                tokens[e] = (words[:, cols], planes[:, cols])
+        grouped = [held.tile([P, C, 4], BF16, name=f"grouped{e}", align_bytes=64) for e in range(E)]
+
+        def gather(e, j):
+            window = planes[j][:].indirect(slots(e * C, (e + 1) * C))
+            if e < 2:
+                nc.vector.tensor_copy(grouped[e][:, :, j], window)
+            else:
+                nc.scalar.activation(grouped[e][:, :, j], window, COPY)
+
+        def quantise(e):
+            words = held.tile([P, C], U32, name=f"words{e}", align_bytes=64)
+            bytes_e = held.tile([P, C], U8, name=f"bytes{e}", align_bytes=64)
+            nc.vector.quantize_mx(
+                out=words[:].bitcast(FP8X4), scales=bytes_e[:], in_=grouped[e][:].rearrange("p c j -> p (c j)")
+            )
+            tokens[e] = (words[:], bytes_e[:])
 
         def multiply1(e, acc, words, sc):
             nc.tensor.matmul_mx(
@@ -200,9 +186,11 @@ def tile_moe_res_glu_relu_kernel(
                 add(out=o[:, a:b], in0=windows[t][:, a:b], in1=res[:, t, a:b], op=ADD)
                 nc.sync.dma_start(out[t * P : (t + 1) * P, a:b], o[:, a:b])
 
-        gather(0, 1)
-        gather(1, 2)
-        gather(2, 4)
+        for j in range(4):
+            for e in range(E):
+                gather(e, j)
+        for e in range(E):
+            quantise(e)
         for e0 in (0, 2):
             for e in (e0, e0 + 1):
                 rectify(e, banks[2 * e0 + e % 2])

@@ -57,10 +57,10 @@ def tile_moe_res_glu_relu_kernel(
         x_rows = xT.rearrange("(p j) t -> p j t", j=4)
 
         def load_scales(tile, src):
-            for g in range(4):
+            for q in range(4):
                 nc.sync.dma_start(
-                    tile[32 * g : 32 * g + 4, :, :].bitcast(I32),
-                    src[:, 0, 4 * g : 4 * g + 4, :].rearrange("e q i -> q e i").bitcast(I32),
+                    tile[q:P:32, :, :].bitcast(I32),
+                    src[:, 0, q:16:4, :].rearrange("e g i -> g e i").bitcast(I32),
                 )
 
         def load_words(words, name, src, e0, e1):

@@ -73,8 +73,9 @@ def tile_moe_res_glu_relu_kernel(
 
         nc.sync.dma_start(offsets[:], offs)
         for j in range(4):
+            if j == 2:
+                load_scales(w1s, w1_scales)
             nc.sync.dma_start(planes[j][:], x_rows[:, j, :])
-        load_scales(w1s, w1_scales)
         load_words(w1w, "w1", w1_words, 0, 2)
         load_words(w3w, "w3", w3_words, 0, 2)
         load_scales(w3s, w3_scales)
@@ -94,22 +95,30 @@ def tile_moe_res_glu_relu_kernel(
         hidden_mx = {}
         rectified = {}
 
-        grouped = [held.tile([P, C, 4], BF16, name=f"grouped{e}", align_bytes=64) for e in range(E)]
+        grouped = {}
+        for e0, e1 in ((0, 1), (1, 2), (2, 4)):
+            grouped[e0] = held.tile([P, (e1 - e0) * C, 4], BF16, name=f"grouped{e0}", align_bytes=64)
 
-        def gather(e, j):
-            window = planes[j][:].indirect(slots(e * C, (e + 1) * C))
-            if e < 2:
-                nc.vector.tensor_copy(grouped[e][:, :, j], window)
-            else:
-                nc.scalar.activation(grouped[e][:, :, j], window, COPY)
+        def gathered(e0, e1, j):
+            first = min(e0, 2)
+            target = grouped[first][:, (e0 - first) * C : (e1 - first) * C, j]
+            return target, planes[j][:].indirect(slots(e0 * C, e1 * C))
 
-        def quantise(e):
-            words = held.tile([P, C], U32, name=f"words{e}", align_bytes=64)
-            bytes_e = held.tile([P, C], U8, name=f"bytes{e}", align_bytes=64)
+        def gather_by_vector(e0, e1, j):
+            nc.vector.tensor_copy(*gathered(e0, e1, j))
+
+        def gather_by_scalar(e0, e1, j):
+            nc.scalar.activation(*gathered(e0, e1, j), COPY)
+
+        def quantise(e0, e1):
+            words = held.tile([P, (e1 - e0) * C], U32, name=f"words{e0}", align_bytes=64)
+            scale_bytes = held.tile([P, (e1 - e0) * C], U8, name=f"scale_bytes{e0}", align_bytes=64)
             nc.vector.quantize_mx(
-                out=words[:].bitcast(FP8X4), scales=bytes_e[:], in_=grouped[e][:].rearrange("p c j -> p (c j)")
+                out=words[:].bitcast(FP8X4), scales=scale_bytes[:], in_=grouped[e0][:].rearrange("p c j -> p (c j)")
             )
-            tokens[e] = (words[:], bytes_e[:])
+            for e in range(e0, e1):
+                cols = slice((e - e0) * C, (e - e0 + 1) * C)
+                tokens[e] = (words[:, cols], scale_bytes[:, cols])
 
         def multiply1(e, acc, words, sc):
             nc.tensor.matmul_mx(
@@ -186,16 +195,26 @@ def tile_moe_res_glu_relu_kernel(
                 add(out=o[:, a:b], in0=windows[t][:, a:b], in1=res[:, t, a:b], op=ADD)
                 nc.sync.dma_start(out[t * P : (t + 1) * P, a:b], o[:, a:b])
 
-        for j in range(4):
-            for e in range(E):
-                gather(e, j)
-        for e in range(E):
-            quantise(e)
-        for e0 in (0, 2):
-            for e in (e0, e0 + 1):
-                rectify(e, banks[2 * e0 + e % 2])
-            for e in (e0, e0 + 1):
-                gate_units(e, banks[2 * e0 + 2 + e % 2])
+        for j in (0, 1):
+            gather_by_vector(0, 1, j)
+            gather_by_vector(2, 3, j)
+            gather_by_scalar(1, 2, j)
+            gather_by_scalar(3, 4, j)
+        for j in (2, 3):
+            gather_by_vector(0, 1, j)
+            gather_by_scalar(1, 2, j)
+            gather_by_scalar(2, 4, j)
+        quantise(0, 1)
+        quantise(1, 2)
+        quantise(2, 4)
+        rectify(0, banks[0])
+        gate_units(0, banks[2])
+        rectify(1, banks[1])
+        gate_units(1, banks[3])
+        rectify(2, banks[4])
+        rectify(3, banks[5])
+        gate_units(2, banks[6])
+        gate_units(3, banks[7])
         turn(0, banks[4])
         turn(1, banks[0])
         turn(2, banks[1])

@@ -6,8 +6,8 @@ from concourse.masks import make_identity
 K, T, E, C, H, N = 512, 640, 4, 128, 512, 512
 P = 128
 NT = N // P
-SHARED_SPLIT = 96
-WIDE = 704
+SHARED_SPLIT = 128
+WIDTHS = (T, 704, T, 1024)
 LAST_PARTS = ((0, 256), (256, 512), (512, T))
 HALVES = ((0, T // 2), (T // 2, T))
 
@@ -47,10 +47,12 @@ def tile_moe_res_glu_relu_kernel(
         w2s = held.tile([P, E, N], U8, name="w2s", align_bytes=64)
         res = held.tile([P, NT, T], F32, name="res")
         planes = [held.tile([P, T], F32, name=f"plane{j}", align_bytes=64) for j in range(4)]
-        windows = [held.tile([P, WIDE if t == 1 else T], F32, name=f"window{t}") for t in range(NT)]
+        windows = [held.tile([P, WIDTHS[t]], F32, name=f"window{t}") for t in range(NT)]
 
         make_identity(nc, ident[:])
         nc.vector.memset(warm[:], 0.0)
+        ones = held.tile([P, 1], F32, name="ones")
+        nc.vector.memset(ones[:], 1.0)
         for t in range(NT):
             nc.vector.memset(windows[t][:, 0:T], 0.0)
 
@@ -71,11 +73,11 @@ def tile_moe_res_glu_relu_kernel(
 
         nc.scalar.activation(out=warm[:], in_=warm[:], func=RELU)
 
+        nc.sync.dma_start(planes[0][:], x_rows[:, 0, :])
         nc.sync.dma_start(offsets[:], offs)
-        for j in range(4):
-            if j == 2:
-                load_scales(w1s, w1_scales)
+        for j in range(1, 4):
             nc.sync.dma_start(planes[j][:], x_rows[:, j, :])
+        load_scales(w1s, w1_scales)
         load_words(w1w, "w1", w1_words, 0, 2)
         load_words(w3w, "w3", w3_words, 0, 2)
         load_scales(w3s, w3_scales)
@@ -96,13 +98,11 @@ def tile_moe_res_glu_relu_kernel(
         rectified = {}
 
         grouped = {}
-        for e0, e1 in ((0, 1), (1, 2), (2, 4)):
-            grouped[e0] = held.tile([P, (e1 - e0) * C, 4], BF16, name=f"grouped{e0}", align_bytes=64)
+        for e in range(3):
+            grouped[e] = held.tile([P, C, 4], BF16, name=f"grouped{e}", align_bytes=64)
 
         def gathered(e0, e1, j):
-            first = min(e0, 2)
-            target = grouped[first][:, (e0 - first) * C : (e1 - first) * C, j]
-            return target, planes[j][:].indirect(slots(e0 * C, e1 * C))
+            return grouped[e0][:, :, j], planes[j][:].indirect(slots(e0 * C, e1 * C))
 
         def gather_by_vector(e0, e1, j):
             nc.vector.tensor_copy(*gathered(e0, e1, j))
@@ -199,46 +199,58 @@ def tile_moe_res_glu_relu_kernel(
             gather_by_vector(0, 1, j)
             gather_by_vector(2, 3, j)
             gather_by_scalar(1, 2, j)
-            gather_by_scalar(3, 4, j)
         for j in (2, 3):
             gather_by_vector(0, 1, j)
             gather_by_scalar(1, 2, j)
-            gather_by_scalar(2, 4, j)
+            gather_by_scalar(2, 3, j)
         quantise(0, 1)
         quantise(1, 2)
-        quantise(2, 4)
+        quantise(2, 3)
+        grouped[3] = held.tile([P, C, 4], BF16, name="grouped0", align_bytes=64)
+        for j in (0, 1):
+            gather_by_scalar(3, 4, j)
+            gather_by_vector(3, 4, j + 2)
+        quantise(3, 4)
         rectify(0, banks[0])
-        gate_units(0, banks[2])
         rectify(1, banks[1])
+        gate_units(0, banks[2])
         gate_units(1, banks[3])
         rectify(2, banks[4])
         rectify(3, banks[5])
         gate_units(2, banks[6])
         gate_units(3, banks[7])
         turn(0, banks[4])
+        multiply2(0, 0, banks[2])
+        apply_gate(0, 0, 1, banks[2])
         turn(1, banks[0])
         turn(2, banks[1])
         turn(3, banks[5])
-        early = {0: banks[2], 1: banks[3], 2: banks[4], 3: banks[0]}
+        early = {1: banks[3], 2: banks[4], 3: banks[0]}
         late = {0: banks[6], 1: banks[7], 2: banks[1], 3: banks[5]}
-        for t in range(NT):
+        def gate_by_gpsimd(t, e0, e1, bank):
+            cols = slice(e0 * C, e1 * C)
+            plain = held.tile([P, (e1 - e0) * C], F32, name=f"plain{t}")
+            nc.scalar.copy(out=plain[:], in_=bank[:, cols])
+            nc.gpsimd.tensor_tensor(out=values[t][:, cols], in0=plain[:], in1=gate_t[:, cols], op=MULT)
+
+        for t in range(1, NT):
             for e in (0, 1):
                 multiply2(t, e, early[t])
             if t in (1, 2):
-                plain = held.tile([P, 2 * C], F32, name=f"plain{t}")
-                nc.scalar.copy(out=plain[:], in_=early[t][:, 0 : 2 * C])
-                nc.gpsimd.tensor_tensor(out=values[t][:, 0 : 2 * C], in0=plain[:], in1=gate_t[:, 0 : 2 * C], op=MULT)
+                gate_by_gpsimd(t, 0, 2, early[t])
             else:
                 apply_gate(t, 0, 2, early[t])
         for t in range(NT):
-            for e in (2, 3):
+            first = 1 if t == 0 else 2
+            for e in range(first, E):
                 multiply2(t, e, late[t])
-            apply_gate(t, 2, 4, late[t])
-        scatter_by_scalar(0, 0, 2 * C)
-        scatter_by_scalar(0, 2 * C, 4 * C)
+            if t != 3:
+                apply_gate(t, first, E, late[t])
+        scatter_by_scalar(0, 0, C)
+        gate_by_gpsimd(3, 2, 4, late[3])
+        scatter_by_scalar(0, C, 4 * C)
         scatter_by_scalar(2, 0, SHARED_SPLIT)
-        scatter_by_scalar(3, 0, 3 * C)
-        scatter_by_scalar(3, 3 * C, 4 * C)
+        nc.scalar.activation(windows[3][:].indirect(slots(0, 4 * C)), values[3][:], COPY, scale=ones[:])
         scatter_by_vector(1, 0, 4 * C)
         scatter_by_vector(2, SHARED_SPLIT, 4 * C)
         add_and_store(nc.gpsimd.tensor_tensor, 0, ((0, T),), held.tile([P, T], F32, name="sum0"))

@@ -8,8 +8,8 @@ P = 128
 NT = N // P
 SHARED_SPLIT = 128
 WIDTHS = (T, 704, T, 1024)
-LAST_PARTS = ((0, 256), (256, 512), (512, T))
-HALVES = ((0, T // 2), (T // 2, T))
+LAST_PARTS = ((448, T), (0, 256), (256, 448))
+JOINT = 448
 
 FLOPS = 3 * 2 * E * C * K * H
 BYTES = 2 * K * T * 4 + N * T * 4 + 3 * E * (P * 1024 + 16 * 512) + E * C * 4 + P * 64
@@ -190,10 +190,12 @@ def tile_moe_res_glu_relu_kernel(
         def scatter_by_scalar(t, a, b):
             nc.scalar.activation(windows[t][:].indirect(slots(a, b)), values[t][:, a:b], COPY)
 
-        def add_and_store(add, t, parts, o):
-            for a, b in parts:
-                add(out=o[:, a:b], in0=windows[t][:, a:b], in1=res[:, t, a:b], op=ADD)
-                nc.sync.dma_start(out[t * P : (t + 1) * P, a:b], o[:, a:b])
+        def add_residual(add, t, a, b, into):
+            add(out=into, in0=windows[t][:, a:b], in1=res[:, t, a:b], op=ADD)
+
+        def add_and_store(add, t, a, b, into):
+            add_residual(add, t, a, b, into)
+            nc.sync.dma_start(out[t * P : (t + 1) * P, a:b], into)
 
         for j in (0, 1):
             gather_by_vector(0, 1, j)
@@ -253,7 +255,13 @@ def tile_moe_res_glu_relu_kernel(
         nc.scalar.activation(windows[3][:].indirect(slots(0, 4 * C)), values[3][:], COPY, scale=ones[:])
         scatter_by_vector(1, 0, 4 * C)
         scatter_by_vector(2, SHARED_SPLIT, 4 * C)
-        add_and_store(nc.gpsimd.tensor_tensor, 0, ((0, T),), held.tile([P, T], F32, name="sum0"))
-        add_and_store(nc.gpsimd.tensor_tensor, 1, ((0, T),), held.tile([P, T], F32, name="sum1"))
-        add_and_store(nc.vector.tensor_tensor, 2, HALVES, res[:, 1, :])
-        add_and_store(nc.vector.tensor_tensor, 3, LAST_PARTS, held.tile([P, T], F32, name="window1"))
+        add_and_store(nc.gpsimd.tensor_tensor, 0, 0, T, held.tile([P, T], F32, name="sum0")[:])
+        add_and_store(nc.gpsimd.tensor_tensor, 1, 0, JOINT, held.tile([P, JOINT], F32, name="sum1")[:])
+        rest = T - JOINT
+        pair = res[:, 1, 0 : 2 * rest].rearrange("p (t c) -> p t c", t=2)
+        add_residual(nc.vector.tensor_tensor, 1, JOINT, T, pair[:, 0, :])
+        add_residual(nc.vector.tensor_tensor, 2, JOINT, T, pair[:, 1, :])
+        nc.sync.dma_start(out[P : 3 * P, JOINT:T].rearrange("(t p) c -> p t c", p=P), pair)
+        add_and_store(nc.vector.tensor_tensor, 2, 0, JOINT, windows[1][:, 0:JOINT])
+        for a, b in LAST_PARTS:
+            add_and_store(nc.vector.tensor_tensor, 3, a, b, windows[2][:, a:b])

from contextlib import ExitStack

import concourse.mybir as mybir
from concourse.masks import make_identity

K, T, E, C, H, N = 512, 640, 4, 128, 512, 512
P = 128
NT = N // P
SHARED_SPLIT = 128
WIDTHS = (T, 704, T, 1024)
LAST_PARTS = ((448, T), (0, 256), (256, 448))
JOINT = 448

FLOPS = 3 * 2 * E * C * K * H
BYTES = 2 * K * T * 4 + N * T * 4 + 3 * E * (P * 1024 + 16 * 512) + E * C * 4 + P * 64

F32 = mybir.dt.float32
BF16 = mybir.dt.bfloat16
U32 = mybir.dt.uint32
I32 = mybir.dt.int32
U16 = mybir.dt.uint16
U8 = mybir.dt.uint8
FP8X4 = mybir.dt.float8_e4m3fn_x4
FP4X4 = mybir.dt.float4_e2m1fn_x4
ADD = mybir.AluOpType.add
MULT = mybir.AluOpType.mult
RELU = mybir.ActivationFunctionType.Relu
COPY = mybir.ActivationFunctionType.Copy


def tile_moe_res_glu_relu_kernel(
    tc, xT, xr, w1_words, w1_scales, w3_words, w3_scales, w2_words, w2_scales, gate, offs, out
):
    nc = tc.nc
    with ExitStack() as ctx:
        held = ctx.enter_context(tc.tile_pool(name="held", bufs=1))
        psum = ctx.enter_context(tc.psum_pool(name="psum", bufs=1))
        banks = [psum.tile([P, 512], F32, name=f"bank{i}") for i in range(8)]

        offsets = held.tile([P, E * C // 16], U16, name="offsets")
        gate_t = held.tile([P, E * C], F32, name="gate_t")
        ident = held.tile([P, P], F32, name="ident")
        warm = held.tile([P, 1], F32, name="warm")
        w1w, w3w, w2w = {}, {}, {}
        w1s = held.tile([P, E, H], U8, name="w1s", align_bytes=64)
        w3s = held.tile([P, E, H], U8, name="w3s", align_bytes=64)
        w2s = held.tile([P, E, N], U8, name="w2s", align_bytes=64)
        res = held.tile([P, NT, T], F32, name="res")
        planes = [held.tile([P, T], F32, name=f"plane{j}", align_bytes=64) for j in range(4)]
        windows = [held.tile([P, WIDTHS[t]], F32, name=f"window{t}") for t in range(NT)]

        make_identity(nc, ident[:])
        nc.vector.memset(warm[:], 0.0)
        ones = held.tile([P, 1], F32, name="ones")
        nc.vector.memset(ones[:], 1.0)
        for t in range(NT):
            nc.vector.memset(windows[t][:, 0:T], 0.0)

        x_rows = xT.rearrange("(p j) t -> p j t", j=4)

        def load_scales(tile, src):
            for q in range(4):
                nc.sync.dma_start(
                    tile[q:P:32, :, :].bitcast(I32),
                    src[:, 0, q:16:4, :].rearrange("e g i -> g e i").bitcast(I32),
                )

        def load_words(words, name, src, e0, e1):
            tile = held.tile([P, e1 - e0, 2 * H], U8, name=f"{name}_{e0}", align_bytes=64)
            nc.sync.dma_start(tile[:].bitcast(I32), src[e0:e1, 0].rearrange("e p n -> p e n").bitcast(I32))
            for e in range(e0, e1):
                words[e] = tile[:, e - e0, :]

        nc.scalar.activation(out=warm[:], in_=warm[:], func=RELU)

        nc.sync.dma_start(planes[0][:], x_rows[:, 0, :])
        nc.sync.dma_start(offsets[:], offs)
        for j in range(1, 4):
            nc.sync.dma_start(planes[j][:], x_rows[:, j, :])
        load_scales(w1s, w1_scales)
        load_words(w1w, "w1", w1_words, 0, 2)
        load_words(w3w, "w3", w3_words, 0, 2)
        load_scales(w3s, w3_scales)
        load_words(w1w, "w1", w1_words, 2, 4)
        load_words(w3w, "w3", w3_words, 2, 4)
        nc.sync.dma_start(gate_t[:], gate[0:P, :])
        load_words(w2w, "w2", w2_words, 0, 2)
        load_scales(w2s, w2_scales)
        load_words(w2w, "w2", w2_words, 2, 4)
        nc.sync.dma_start(res[:], xr.rearrange("(t p) c -> p t c", p=P))

        def slots(a, b):
            return offsets[:, a // 16 : b // 16]

        tokens = {}
        hidden = {}
        hidden_mx = {}
        rectified = {}

        grouped = {}
        for e in range(3):
            grouped[e] = held.tile([P, C, 4], BF16, name=f"grouped{e}", align_bytes=64)

        def gathered(e0, e1, j):
            return grouped[e0][:, :, j], planes[j][:].indirect(slots(e0 * C, e1 * C))

        def gather_by_vector(e0, e1, j):
            nc.vector.tensor_copy(*gathered(e0, e1, j))

        def gather_by_scalar(e0, e1, j):
            nc.scalar.activation(*gathered(e0, e1, j), COPY)

        def quantise(e0, e1):
            words = held.tile([P, (e1 - e0) * C], U32, name=f"words{e0}", align_bytes=64)
            scale_bytes = held.tile([P, (e1 - e0) * C], U8, name=f"scale_bytes{e0}", align_bytes=64)
            nc.vector.quantize_mx(
                out=words[:].bitcast(FP8X4), scales=scale_bytes[:], in_=grouped[e0][:].rearrange("p c j -> p (c j)")
            )
            for e in range(e0, e1):
                cols = slice((e - e0) * C, (e - e0 + 1) * C)
                tokens[e] = (words[:, cols], scale_bytes[:, cols])

        def multiply1(e, acc, words, sc):
            nc.tensor.matmul_mx(
                out=acc[:],
                lhsT=tokens[e][0].bitcast(FP8X4),
                lhsT_scale=tokens[e][1],
                rhs=words[e].bitcast(FP4X4),
                rhs_scale=sc[:, e, :],
                start=True,
                stop=True,
            )

        def pairs_of(acc):
            return acc[:].rearrange("s (p u d) -> s u p d", u=2, d=2)

        def halves(e):
            return (slice(0, 1), slice(1, 2)) if e >= 2 else (slice(0, 2),)

        def rectify(e, bank):
            multiply1(e, bank, w1w, w1s)
            ra = held.tile([P, 2, P, 2], F32, name=f"ra{e}")
            for us in halves(e):
                nc.scalar.activation(out=ra[:, us], in_=pairs_of(bank)[:, us], func=RELU)
            rectified[e] = ra

        def gate_units(e, bank):
            multiply1(e, bank, w3w, w3s)
            h = held.tile([P, 2, P, 2], BF16, name=f"h{e}", align_bytes=64)[:]
            for us in halves(e):
                nc.vector.tensor_tensor(out=h[:, us], in0=pairs_of(bank)[:, us], in1=rectified[e][:, us], op=MULT)
            hidden[e] = h

        def turn(e, bank):
            ph = bank[:, 0 : 2 * C].rearrange("p (u c) -> p u c", u=2)
            for u in range(2):
                pairs = hidden[e][:, u, :, :].rearrange("s p d -> s (p d)").bitcast(F32)
                nc.tensor.transpose(ph[:, u, :], pairs, ident[:])
            hg = held.tile([P, C, 4], BF16, name=f"hg{e}", align_bytes=64)
            nc.scalar.copy(
                out=hg[:].rearrange("p c j -> p (c j)").bitcast(F32).rearrange("p (c u) -> p c u", u=2),
                in_=ph.rearrange("p u c -> p c u"),
            )
            hc = held.tile([P, C], U32, name=f"hc{e}", align_bytes=64)
            hs = held.tile([P, C], U8, name=f"hs{e}", align_bytes=64)
            nc.vector.quantize_mx(out=hc[:].bitcast(FP8X4), scales=hs[:], in_=hg[:].rearrange("p c j -> p (c j)"))
            hidden_mx[e] = (hc, hs)

        values = [held.tile([P, E * C], F32, name=f"values{t}") for t in range(NT)]

        def multiply2(t, e, bank):
            hc, hs = hidden_mx[e]
            nc.tensor.matmul_mx(
                out=bank[:, e * C : (e + 1) * C],
                lhsT=w2w[e][:, t * 2 * P : (t + 1) * 2 * P].bitcast(FP4X4),
                lhsT_scale=w2s[:, e, t * P : (t + 1) * P],
                rhs=hc[:].bitcast(FP8X4),
                rhs_scale=hs[:],
                start=True,
                stop=True,
            )

        def apply_gate(t, e0, e1, bank):
            cols = slice(e0 * C, e1 * C)
            nc.vector.tensor_tensor(out=values[t][:, cols], in0=bank[:, cols], in1=gate_t[:, cols], op=MULT)

        def scatter_by_vector(t, a, b):
            nc.vector.tensor_copy(windows[t][:].indirect(slots(a, b)), values[t][:, a:b])

        def scatter_by_scalar(t, a, b):
            nc.scalar.activation(windows[t][:].indirect(slots(a, b)), values[t][:, a:b], COPY)

        def add_residual(add, t, a, b, into):
            add(out=into, in0=windows[t][:, a:b], in1=res[:, t, a:b], op=ADD)

        def add_and_store(add, t, a, b, into):
            add_residual(add, t, a, b, into)
            nc.sync.dma_start(out[t * P : (t + 1) * P, a:b], into)

        for j in (0, 1):
            gather_by_vector(0, 1, j)
            gather_by_vector(2, 3, j)
            gather_by_scalar(1, 2, j)
        for j in (2, 3):
            gather_by_vector(0, 1, j)
            gather_by_scalar(1, 2, j)
            gather_by_scalar(2, 3, j)
        quantise(0, 1)
        quantise(1, 2)
        quantise(2, 3)
        grouped[3] = held.tile([P, C, 4], BF16, name="grouped0", align_bytes=64)
        for j in (0, 1):
            gather_by_scalar(3, 4, j)
            gather_by_vector(3, 4, j + 2)
        quantise(3, 4)
        rectify(0, banks[0])
        rectify(1, banks[1])
        gate_units(0, banks[2])
        gate_units(1, banks[3])
        rectify(2, banks[4])
        rectify(3, banks[5])
        gate_units(2, banks[6])
        gate_units(3, banks[7])
        turn(0, banks[4])
        multiply2(0, 0, banks[2])
        apply_gate(0, 0, 1, banks[2])
        turn(1, banks[0])
        turn(2, banks[1])
        turn(3, banks[5])
        early = {1: banks[3], 2: banks[4], 3: banks[0]}
        late = {0: banks[6], 1: banks[7], 2: banks[1], 3: banks[5]}
        def gate_by_gpsimd(t, e0, e1, bank):
            cols = slice(e0 * C, e1 * C)
            plain = held.tile([P, (e1 - e0) * C], F32, name=f"plain{t}")
            nc.scalar.copy(out=plain[:], in_=bank[:, cols])
            nc.gpsimd.tensor_tensor(out=values[t][:, cols], in0=plain[:], in1=gate_t[:, cols], op=MULT)

        for t in range(1, NT):
            for e in (0, 1):
                multiply2(t, e, early[t])
            if t in (1, 2):
                gate_by_gpsimd(t, 0, 2, early[t])
            else:
                apply_gate(t, 0, 2, early[t])
        for t in range(NT):
            first = 1 if t == 0 else 2
            for e in range(first, E):
                multiply2(t, e, late[t])
            if t != 3:
                apply_gate(t, first, E, late[t])
        scatter_by_scalar(0, 0, C)
        gate_by_gpsimd(3, 2, 4, late[3])
        scatter_by_scalar(0, C, 4 * C)
        scatter_by_scalar(2, 0, SHARED_SPLIT)
        nc.scalar.activation(windows[3][:].indirect(slots(0, 4 * C)), values[3][:], COPY, scale=ones[:])
        scatter_by_vector(1, 0, 4 * C)
        scatter_by_vector(2, SHARED_SPLIT, 4 * C)
        add_and_store(nc.gpsimd.tensor_tensor, 0, 0, T, held.tile([P, T], F32, name="sum0")[:])
        add_and_store(nc.gpsimd.tensor_tensor, 1, 0, JOINT, held.tile([P, JOINT], F32, name="sum1")[:])
        rest = T - JOINT
        pair = res[:, 1, 0 : 2 * rest].rearrange("p (t c) -> p t c", t=2)
        add_residual(nc.vector.tensor_tensor, 1, JOINT, T, pair[:, 0, :])
        add_residual(nc.vector.tensor_tensor, 2, JOINT, T, pair[:, 1, :])
        nc.sync.dma_start(out[P : 3 * P, JOINT:T].rearrange("(t p) c -> p t c", p=P), pair)
        add_and_store(nc.vector.tensor_tensor, 2, 0, JOINT, windows[1][:, 0:JOINT])
        for a, b in LAST_PARTS:
            add_and_store(nc.vector.tensor_tensor, 3, a, b, windows[2][:, a:b])
